import numpy as np
import ml_dtypes


def mxq(x, axis, fmt="e4m3"):
    dtype, down = {"e4m3": (ml_dtypes.float8_e4m3fn, 7), "e5m2": (ml_dtypes.float8_e5m2, 14)}[fmt]
    v = np.moveaxis(np.asarray(x, np.float32).astype(ml_dtypes.bfloat16).astype(np.float64), axis, -1)
    blocks = v.reshape(v.shape[:-1] + (-1, 32))
    amax = np.abs(blocks).max(-1, keepdims=True)
    byte = np.maximum(np.where(amax > 0, np.frexp(amax)[1] - 1 + 127, 0) - down, 1)
    scale = np.exp2(byte - 127.0)
    codes = (blocks / scale).astype(np.float32).astype(dtype).astype(np.float64)
    return np.moveaxis((codes * scale).reshape(v.shape), -1, axis)


WIDE = False


def mx_kscale(k):
    if not WIDE:
        return np.ones(k)
    levels = np.array([10, -10, 5, -5, 0])
    if k % 512:
        return np.exp2(np.random.permutation(np.resize(levels, k // 32))).repeat(32)
    a = np.empty((k // 512, 16))
    for p in range(k // 512):
        a[p, :8] = np.random.permutation(np.resize(levels, 8))
        for g in range(8):
            far = levels[np.abs(levels - a[p, g]) >= 10]
            a[p, g + 8] = far[np.random.randint(len(far))]
    return np.exp2(a.ravel()).repeat(32)


def f64(x):
    return np.asarray(x).astype(np.float64)


def striped(idx):
    return np.tile(idx.reshape(-1, 16).T, (8, 1)).astype(np.uint16)


def unstriped(offs):
    return offs[:16].T.reshape(-1).astype(np.int64)


def striped8(idx):
    return np.concatenate([x.reshape(-1, 16).T for x in idx]).astype(np.uint16)


def runs(offs, k):
    lists = np.stack([offs[16 * r : 16 * r + 16].T.reshape(-1) for r in range(8)]).astype(np.int64)
    return lists[np.arange(k) % 512 // 64]


def pack_weight(w):
    k, n = w.shape
    w = f64(np.asarray(w, np.float32).astype(ml_dtypes.bfloat16)).reshape(k // 32, 32, n)
    amax = np.abs(w).max(1)
    byte = np.clip(np.where(amax > 0, np.frexp(amax)[1] - 1 + 127 - 7, 1), 1, 254)
    scaled = (w * np.exp2(127.0 - byte)[:, None, :]).reshape(k, n).astype(np.float32)
    words = np.ascontiguousarray(scaled.reshape(k // 512, 128, 4, n).transpose(0, 1, 3, 2)).astype(ml_dtypes.float8_e4m3fn).view(np.uint8)
    return words, np.ascontiguousarray(byte.astype(np.uint8).reshape(k // 512, 16, n))


def unpack_weight(words, scales):
    g, p, n, _ = words.shape
    vals = np.ascontiguousarray(words).view(ml_dtypes.float8_e4m3fn).astype(np.float64) * np.repeat(np.exp2(scales.astype(np.float64) - 127.0), 8, axis=1)[..., None]
    return vals.transpose(0, 1, 3, 2).reshape(g * 512, n)


def sigmoid(v):
    return 1.0 / (1.0 + np.exp(-np.maximum(v, -700.0)))

def planes(y):
    n, m = y.shape
    v = y.astype(np.float32).astype(ml_dtypes.bfloat16).astype(np.float64).reshape(n // 32, 32, m)
    top = np.abs(v).max(1)
    byte = np.clip(np.where(top > 0, np.frexp(top)[1] - 1 + 127 - 7, 1), 1, 254)
    codes = (v * np.exp2(127.0 - byte)[:, None, :]).reshape(n, m).astype(np.float32).astype(ml_dtypes.float8_e4m3fn).view(np.uint8)
    words = codes.reshape(n // 512, 128, 4, m).transpose(0, 1, 3, 2)
    return np.ascontiguousarray(words), np.ascontiguousarray(byte.astype(np.uint8).reshape(n // 512, 16, m))


K, T, S, N = 512, 2048, 512, 512


def setup_inputs():
    n = np.random.standard_normal
    s = mx_kscale(K)[:, None]
    packed_xT = pack_weight(n((K, T)) * s)
    return {
        "x_words": packed_xT[0],
        "x_scales": packed_xT[1],
        "w1": (n((K, N)) / np.sqrt(K) / s).astype(np.float32),
        "w2": (n((K, N)) / np.sqrt(K) / s).astype(np.float32),
        "st": n((N, S)).astype(np.float32),
        "offs": striped(np.random.permutation(T)[:S]),
        "par": striped8(np.random.randint(0, S, (8, S))),
    }


def reference(x_words, x_scales, w1, w2, st, offs, par):
    sp = f64(st)[np.arange(N)[:, None], runs(par, N)]
    xq = unpack_weight(x_words, x_scales)[:, unstriped(offs)]
    f = sigmoid(mxq(f64(w1), 0, "e4m3").T @ xq)
    c = mxq(f64(w2), 0, "e4m3").T @ xq
    out_0 = sp + f * (c - sp)
    return (out_0,) + planes(out_0)

@@ -1,0 +1,175 @@
+from contextlib import ExitStack
+
+import concourse.mybir as mybir
+
+K, T, S, N = 512, 2048, 512, 512
+FLOPS = 2 * 2 * K * N * S
+
+F32 = mybir.dt.float32
+BF16 = mybir.dt.bfloat16
+I32 = mybir.dt.int32
+U32 = mybir.dt.uint32
+U16 = mybir.dt.uint16
+U8 = mybir.dt.uint8
+FP8X4 = mybir.dt.float8_e4m3fn_x4
+ALU = mybir.AluOpType
+ACT = mybir.ActivationFunctionType
+
+P = 128
+PACK = 4
+HALF = S // 2
+QUARTER = S // 4
+
+
+def tile_picked_mingru8_none_po_kernel(tc, x_words, x_scales, w1, w2, st, offs, par, out_0, out_1, out_2):
+    nc = tc.nc
+    with ExitStack() as ctx:
+        sb = ctx.enter_context(tc.tile_pool(name="sb", bufs=1))
+        ps = ctx.enter_context(tc.psum_pool(name="ps", bufs=1))
+
+        par_t = sb.tile([P, S // 16], U16, name="par_t")
+        offs_t = sb.tile([P, S // 16], U16, name="offs_t")
+        x_w = sb.tile([P, T], U32, name="x_w", align_bytes=64)
+        x_s = sb.tile([P, T], U8, name="x_s", align_bytes=64)
+        st_t = [sb.tile([P, S], F32, name="st%d" % t, align_bytes=64) for t in range(PACK)]
+        raw = [[sb.tile([P, PACK, HALF], F32, name="raw%d%d" % (w, h), align_bytes=64) for h in range(2)] for w in range(2)]
+        st_rows = st.rearrange("(p t) j -> p t j", t=PACK)
+        w_rows = [w.rearrange("(p j) m -> p j m", j=PACK) for w in (w1, w2)]
+
+        def load_w(w, h):
+            nc.sync.dma_start(raw[w][h][:], w_rows[w][:, :, h * HALF : (h + 1) * HALF])
+
+        def load_xs(q):
+            nc.sync.dma_start(x_s[32 * q : 32 * q + 4, :].bitcast(I32), x_scales[0, 4 * q : 4 * q + 4, :].bitcast(I32))
+
+        warm = sb.tile([P, 2], F32, name="warm")
+        nc.vector.memset(x_s[:].bitcast(I32), 0)
+        nc.vector.memset(warm[:, 0:1], 0.0)
+        nc.scalar.activation(warm[:, 1:2], warm[:, 0:1], ACT.Sigmoid)
+
+        nc.sync.dma_start(st_t[0][:], st_rows[:, 0, :])
+        nc.sync.dma_start(par_t[:], par)
+        for t in (1, 2):
+            nc.sync.dma_start(st_t[t][:], st_rows[:, t, :])
+        load_w(1, 0)
+        nc.sync.dma_start(offs_t[:], offs)
+        for q in range(4):
+            load_xs(q)
+        load_w(1, 1)
+        nc.sync.dma_start(x_w[:].bitcast(I32), x_words[0].rearrange("p n r -> p (n r)").bitcast(I32))
+        nc.sync.dma_start(st_t[3][:], st_rows[:, 3, :])
+        load_w(0, 0)
+        load_w(0, 1)
+
+        sp = [sb.tile([P, PACK, HALF], F32, name="sp%d" % h, align_bytes=64) for h in range(2)]
+
+        def gather_state(t):
+            for h in range(2):
+                nc.vector.tensor_copy(sp[h][:, t, :], st_t[t][:].indirect(par_t[:, 16 * h : 16 * (h + 1)]))
+
+        w_bf = [sb.tile([P, PACK * N], BF16, name="w_bf%d" % w, tag="w_bf%d" % w, align_bytes=64) for w in range(2)]
+        w_codes = [sb.tile([P, N], U32, name="w_codes%d" % w, align_bytes=64) for w in range(2)]
+        w_scales = [sb.tile([P, N], U8, name="w_scales%d" % w, align_bytes=64) for w in range(2)]
+
+        def deal(copy, w, h, a, b):
+            dst = w_bf[w][:].rearrange("p (t m j) -> p m j t", t=PACK, j=PACK)[:, 64 * h + a : 64 * h + b]
+            src = raw[w][h][:].rearrange("p j (m t) -> p m j t", t=PACK)[:, a:b]
+            copy(dst, src)
+
+        def quant_w(w, a, b):
+            nc.vector.quantize_mx(
+                out=w_codes[w][:, P * a : P * b].bitcast(FP8X4),
+                scales=w_scales[w][:, P * a : P * b],
+                in_=w_bf[w][:, PACK * P * a : PACK * P * b],
+            )
+
+        xg_w = sb.tile([P, S], U32, name="xg_w", align_bytes=64)
+        xg_s = sb.tile([P, S], U8, name="xg_s", align_bytes=64)
+
+        def product(w, h, tp):
+            bank = ps.tile([P, 2, HALF], F32, name="bank%d%d%d" % (w, h, tp))
+            for i in range(2):
+                t = 2 * tp + i
+                nc.tensor.matmul_mx(
+                    out=bank[:, i, :],
+                    lhsT=w_codes[w][:, P * t : P * (t + 1)].bitcast(FP8X4),
+                    lhsT_scale=w_scales[w][:, P * t : P * (t + 1)],
+                    rhs=xg_w[:, HALF * h : HALF * (h + 1)].bitcast(FP8X4),
+                    rhs_scale=xg_s[:, HALF * h : HALF * (h + 1)],
+                    start=True,
+                    stop=True,
+                )
+            return bank
+
+        for t in range(3):
+            gather_state(t)
+        nc.vector.tensor_copy(xg_s[:], x_s[:].indirect(offs_t[:]))
+        deal(nc.scalar.copy, 1, 0, 0, 64)
+        deal(nc.scalar.copy, 1, 1, 0, 64)
+        quant_w(1, 0, 4)
+        nc.vector.tensor_copy(xg_w[:], x_w[:].indirect(offs_t[:]))
+        order = [(h, tp) for h in range(2) for tp in range(2)]
+        c_bank = {key: product(1, key[0], key[1]) for key in order}
+        gather_state(3)
+
+        deal(nc.scalar.copy, 0, 0, 0, 64)
+        deal(nc.scalar.copy, 0, 1, 0, 22)
+        deal(nc.vector.tensor_copy, 0, 1, 22, 64)
+        quant_w(0, 0, 2)
+        quant_w(0, 2, 4)
+        u_bank = {key: product(0, key[0], key[1]) for key in order}
+
+        diff_first = sb.tile([P, 2, HALF], F32, name="diff_first", align_bytes=64)
+        diff_rest = sb.tile([P, 6, HALF], F32, name="diff_rest", tag="w_bf0", align_bytes=64)
+        diff = {(0, 0): diff_first[:], (0, 1): diff_rest[:, 0:2, :], (1, 0): diff_rest[:, 2:4, :], (1, 1): diff_rest[:, 4:6, :]}
+        gate = [sb.tile([P, PACK, HALF], F32, name="gate%d" % h, align_bytes=64) for h in range(2)]
+        step = [sb.tile([P, PACK, HALF], F32, name="step%d" % h, align_bytes=64) for h in range(2)]
+        for h, tp in order:
+            nc.vector.tensor_tensor(diff[(h, tp)], c_bank[(h, tp)][:], sp[h][:, 2 * tp : 2 * tp + 2, :], ALU.subtract)
+        for h, tp in order:
+            nc.scalar.activation(gate[h][:, 2 * tp : 2 * tp + 2, :], u_bank[(h, tp)][:], ACT.Sigmoid)
+
+        y_codes = sb.tile([P, S], U32, name="y_codes", align_bytes=64)
+        y_scales = sb.tile([P, S], U8, name="y_scales", align_bytes=64)
+        out_rows = out_0.rearrange("(p t) j -> p t j", t=PACK)
+        out_words = out_1[0].rearrange("p n r -> p (n r)").bitcast(I32)
+        widths = [(0, HALF), (HALF, QUARTER), (HALF + QUARTER, QUARTER)]
+        y = [sb.tile([P, PACK, n], F32, name="y%d" % i, align_bytes=64) for i, (j0, n) in enumerate(widths)]
+        y_bf = [sb.tile([P, PACK * n], BF16, name="y_bf%d" % i, align_bytes=64) for i, (j0, n) in enumerate(widths)]
+
+        def weave(copy, i):
+            copy(y_bf[i][:].rearrange("p (c i t) -> p c t i", i=4, t=PACK), y[i][:].rearrange("p t (c i) -> p c t i", i=4))
+
+        def quant_y(i):
+            j0, n = widths[i]
+            nc.vector.quantize_mx(out=y_codes[:, j0 : j0 + n].bitcast(FP8X4), scales=y_scales[:, j0 : j0 + n], in_=y_bf[i][:])
+
+        def store_y(i):
+            j0, n = widths[i]
+            nc.sync.dma_start(out_rows[:, :, j0 : j0 + n], y[i][:])
+
+        for tp in range(2):
+            rows = slice(2 * tp, 2 * tp + 2)
+            nc.vector.tensor_tensor(step[0][:, rows, :], gate[0][:, rows, :], diff[(0, tp)], ALU.mult)
+        for tp in range(2):
+            rows = slice(2 * tp, 2 * tp + 2)
+            nc.vector.tensor_tensor(y[0][:, rows, :], step[0][:, rows, :], sp[0][:, rows, :], ALU.add)
+        store_y(0)
+        weave(nc.scalar.copy, 0)
+        for i in (1, 2):
+            cols = slice(QUARTER * (i - 1), QUARTER * i)
+            nc.vector.tensor_tensor(step[1][:, :, cols], gate[1][:, :, cols], diff_rest[:, 2:6, cols], ALU.mult)
+        for i in (1, 2):
+            cols = slice(QUARTER * (i - 1), QUARTER * i)
+            nc.vector.tensor_tensor(y[i][:], step[1][:, :, cols], sp[1][:, :, cols], ALU.add)
+            store_y(i)
+        weave(nc.scalar.copy, 1)
+        quant_y(0)
+        nc.sync.dma_start(out_words[:, 0:HALF], y_codes[:, 0:HALF].bitcast(I32))
+        weave(nc.vector.tensor_copy, 2)
+        quant_y(1)
+        quant_y(2)
+        nc.sync.dma_start(out_words[:, HALF:S], y_codes[:, HALF:S].bitcast(I32))
+        for q in range(4):
+            queue = nc.scalar if q % 2 == 0 else nc.sync
+            queue.dma_start(out_2[0, 4 * q : 4 * q + 4, :].bitcast(I32), y_scales[32 * q : 32 * q + 4, :].bitcast(I32))

@@ -32,7 +32,7 @@ def tile_picked_mingru8_none_po_kernel(tc, x_words, x_scales, w1, w2, st, offs, 
         x_w = sb.tile([P, T], U32, name="x_w", align_bytes=64)
         x_s = sb.tile([P, T], U8, name="x_s", align_bytes=64)
         st_t = [sb.tile([P, S], F32, name="st%d" % t, align_bytes=64) for t in range(PACK)]
-        raw = [[sb.tile([P, PACK, HALF], F32, name="raw%d%d" % (w, h), align_bytes=64) for h in range(2)] for w in range(2)]
+        raw = [[sb.tile([P, PACK, HALF], F32, name="raw%d%d" % (w, h), tag="raw%d%d" % (w, h), align_bytes=64) for h in range(2)] for w in range(2)]
         st_rows = st.rearrange("(p t) j -> p t j", t=PACK)
         w_rows = [w.rearrange("(p j) m -> p j m", j=PACK) for w in (w1, w2)]
 
@@ -42,10 +42,7 @@ def tile_picked_mingru8_none_po_kernel(tc, x_words, x_scales, w1, w2, st, offs, 
         def load_xs(q):
             nc.sync.dma_start(x_s[32 * q : 32 * q + 4, :].bitcast(I32), x_scales[0, 4 * q : 4 * q + 4, :].bitcast(I32))
 
-        warm = sb.tile([P, 2], F32, name="warm")
         nc.vector.memset(x_s[:].bitcast(I32), 0)
-        nc.vector.memset(warm[:, 0:1], 0.0)
-        nc.scalar.activation(warm[:, 1:2], warm[:, 0:1], ACT.Sigmoid)
 
         nc.sync.dma_start(st_t[0][:], st_rows[:, 0, :])
         nc.sync.dma_start(par_t[:], par)
@@ -57,18 +54,18 @@ def tile_picked_mingru8_none_po_kernel(tc, x_words, x_scales, w1, w2, st, offs, 
             load_xs(q)
         load_w(1, 1)
         nc.sync.dma_start(x_w[:].bitcast(I32), x_words[0].rearrange("p n r -> p (n r)").bitcast(I32))
-        nc.sync.dma_start(st_t[3][:], st_rows[:, 3, :])
         load_w(0, 0)
         load_w(0, 1)
+        nc.sync.dma_start(st_t[3][:], st_rows[:, 3, :])
 
-        sp = [sb.tile([P, PACK, HALF], F32, name="sp%d" % h, align_bytes=64) for h in range(2)]
+        sp = [sb.tile([P, PACK - 1, HALF], F32, name="sp%d" % h, align_bytes=64) for h in range(2)]
 
         def gather_state(t):
             for h in range(2):
                 nc.vector.tensor_copy(sp[h][:, t, :], st_t[t][:].indirect(par_t[:, 16 * h : 16 * (h + 1)]))
 
         w_bf = [sb.tile([P, PACK * N], BF16, name="w_bf%d" % w, tag="w_bf%d" % w, align_bytes=64) for w in range(2)]
-        w_codes = [sb.tile([P, N], U32, name="w_codes%d" % w, align_bytes=64) for w in range(2)]
+        w_codes = {}
         w_scales = [sb.tile([P, N], U8, name="w_scales%d" % w, align_bytes=64) for w in range(2)]
 
         def deal(copy, w, h, a, b):
@@ -76,94 +73,109 @@ def tile_picked_mingru8_none_po_kernel(tc, x_words, x_scales, w1, w2, st, offs, 
             src = raw[w][h][:].rearrange("p j (m t) -> p m j t", t=PACK)[:, a:b]
             copy(dst, src)
 
-        def quant_w(w, a, b):
-            nc.vector.quantize_mx(
-                out=w_codes[w][:, P * a : P * b].bitcast(FP8X4),
-                scales=w_scales[w][:, P * a : P * b],
-                in_=w_bf[w][:, PACK * P * a : PACK * P * b],
-            )
+        def quant_w(w, a, b, tag):
+            codes = sb.tile([P, P * (b - a)], U32, name="w_codes%d%d" % (w, a), tag=tag, align_bytes=64)
+            nc.vector.quantize_mx(out=codes[:].bitcast(FP8X4), scales=w_scales[w][:, P * a : P * b], in_=w_bf[w][:, PACK * P * a : PACK * P * b])
+            for t in range(a, b):
+                w_codes[(w, t)] = codes[:, P * (t - a) : P * (t - a + 1)]
 
-        xg_w = sb.tile([P, S], U32, name="xg_w", align_bytes=64)
+        xg_w = [sb.tile([P, HALF], U32, name="xg_w%d" % h, align_bytes=64) for h in range(2)]
         xg_s = sb.tile([P, S], U8, name="xg_s", align_bytes=64)
 
-        def product(w, h, tp):
-            bank = ps.tile([P, 2, HALF], F32, name="bank%d%d%d" % (w, h, tp))
-            for i in range(2):
-                t = 2 * tp + i
-                nc.tensor.matmul_mx(
-                    out=bank[:, i, :],
-                    lhsT=w_codes[w][:, P * t : P * (t + 1)].bitcast(FP8X4),
-                    lhsT_scale=w_scales[w][:, P * t : P * (t + 1)],
-                    rhs=xg_w[:, HALF * h : HALF * (h + 1)].bitcast(FP8X4),
-                    rhs_scale=xg_s[:, HALF * h : HALF * (h + 1)],
-                    start=True,
-                    stop=True,
-                )
-            return bank
+        def product(bank, w, h, t):
+            nc.tensor.matmul_mx(
+                out=bank[:, t % 2, :],
+                lhsT=w_codes[(w, t)].bitcast(FP8X4),
+                lhsT_scale=w_scales[w][:, P * t : P * (t + 1)],
+                rhs=xg_w[h][:].bitcast(FP8X4),
+                rhs_scale=xg_s[:, HALF * h : HALF * (h + 1)],
+                start=True,
+                stop=True,
+            )
+
+        def scalar_copy(dst, src):
+            nc.scalar.activation(dst, src, ACT.Copy)
 
         for t in range(3):
             gather_state(t)
         nc.vector.tensor_copy(xg_s[:], x_s[:].indirect(offs_t[:]))
-        deal(nc.scalar.copy, 1, 0, 0, 64)
-        deal(nc.scalar.copy, 1, 1, 0, 64)
-        quant_w(1, 0, 4)
-        nc.vector.tensor_copy(xg_w[:], x_w[:].indirect(offs_t[:]))
-        order = [(h, tp) for h in range(2) for tp in range(2)]
-        c_bank = {key: product(1, key[0], key[1]) for key in order}
-        gather_state(3)
+        deal(scalar_copy, 1, 0, 0, 64)
+        deal(scalar_copy, 1, 1, 0, 64)
+        quant_w(1, 0, 4, "codes1")
+        for h in range(2):
+            nc.vector.tensor_copy(xg_w[h][:], x_w[:].indirect(offs_t[:, 16 * h : 16 * (h + 1)]))
+        c_bank = [[ps.tile([P, 2, HALF], F32, name="c_bank%d%d" % (tp, h)) for h in range(2)] for tp in range(2)]
+        for tp in range(2):
+            for h in range(2):
+                for t in (2 * tp, 2 * tp + 1):
+                    product(c_bank[tp][h], 1, h, t)
 
-        deal(nc.scalar.copy, 0, 0, 0, 64)
-        deal(nc.scalar.copy, 0, 1, 0, 22)
-        deal(nc.vector.tensor_copy, 0, 1, 22, 64)
-        quant_w(0, 0, 2)
-        quant_w(0, 2, 4)
-        u_bank = {key: product(0, key[0], key[1]) for key in order}
+        diff = [sb.tile([P, PACK, HALF], F32, name="diff%d" % h, align_bytes=64) for h in range(2)]
+        for h in range(2):
+            nc.vector.tensor_tensor(diff[h][:, 0:2, :], c_bank[0][h][:], sp[h][:, 0:2, :], ALU.subtract)
+        for h in range(2):
+            nc.vector.tensor_tensor(diff[h][:, 2, :], sp[h][:, 2, :], c_bank[1][h][:, 0, :], ALU.subtract)
+        deal(scalar_copy, 0, 0, 0, 64)
+        deal(scalar_copy, 0, 1, 0, 64)
+        quant_w(0, 0, 2, "codes00")
+        quant_w(0, 2, 4, "codes01")
+        c_last = sb.tile([P, 2, HALF], F32, name="c_last", tag="raw01", align_bytes=64)
+        for h in range(2):
+            scalar_copy(c_last[:, h, :], c_bank[1][h][:, 1, :])
+            nc.vector.tensor_tensor(diff[h][:, 3, :], st_t[3][:].indirect(par_t[:, 16 * h : 16 * (h + 1)]), c_last[:, h, :], ALU.subtract)
 
-        diff_first = sb.tile([P, 2, HALF], F32, name="diff_first", align_bytes=64)
-        diff_rest = sb.tile([P, 6, HALF], F32, name="diff_rest", tag="w_bf0", align_bytes=64)
-        diff = {(0, 0): diff_first[:], (0, 1): diff_rest[:, 0:2, :], (1, 0): diff_rest[:, 2:4, :], (1, 1): diff_rest[:, 4:6, :]}
         gate = [sb.tile([P, PACK, HALF], F32, name="gate%d" % h, align_bytes=64) for h in range(2)]
         step = [sb.tile([P, PACK, HALF], F32, name="step%d" % h, align_bytes=64) for h in range(2)]
-        for h, tp in order:
-            nc.vector.tensor_tensor(diff[(h, tp)], c_bank[(h, tp)][:], sp[h][:, 2 * tp : 2 * tp + 2, :], ALU.subtract)
-        for h, tp in order:
-            nc.scalar.activation(gate[h][:, 2 * tp : 2 * tp + 2, :], u_bank[(h, tp)][:], ACT.Sigmoid)
+        for h in range(2):
+            for tp in range(2):
+                u_bank = ps.tile([P, 2, HALF], F32, name="u_bank%d%d" % (tp, h))
+                for t in (2 * tp, 2 * tp + 1):
+                    product(u_bank, 0, h, t)
+                nc.scalar.activation(gate[h][:, 2 * tp : 2 * tp + 2, :], u_bank[:], ACT.Tanh, scale=0.5 if tp == 0 else -0.5)
 
         y_codes = sb.tile([P, S], U32, name="y_codes", align_bytes=64)
         y_scales = sb.tile([P, S], U8, name="y_scales", align_bytes=64)
         out_rows = out_0.rearrange("(p t) j -> p t j", t=PACK)
         out_words = out_1[0].rearrange("p n r -> p (n r)").bitcast(I32)
-        widths = [(0, HALF), (HALF, QUARTER), (HALF + QUARTER, QUARTER)]
-        y = [sb.tile([P, PACK, n], F32, name="y%d" % i, align_bytes=64) for i, (j0, n) in enumerate(widths)]
-        y_bf = [sb.tile([P, PACK * n], BF16, name="y_bf%d" % i, align_bytes=64) for i, (j0, n) in enumerate(widths)]
+        y = [sb.tile([P, PACK, HALF], F32, name="y%d" % h, align_bytes=64) for h in range(2)]
+        pieces = [(0, 0, HALF), (1, 0, QUARTER), (1, QUARTER, HALF)]
+        y_bf = [sb.tile([P, PACK * (b - a)], BF16, name="y_bf%d" % i, align_bytes=64) for i, (h, a, b) in enumerate(pieces)]
 
-        def weave(copy, i):
-            copy(y_bf[i][:].rearrange("p (c i t) -> p c t i", i=4, t=PACK), y[i][:].rearrange("p t (c i) -> p c t i", i=4))
+        def scale_step(h, tp):
+            rows = slice(2 * tp, 2 * tp + 2)
+            nc.vector.scalar_tensor_tensor(step[h][:, rows, :], gate[h][:, rows, :], 1.0, diff[h][:, rows, :], ALU.add, ALU.mult)
 
-        def quant_y(i):
-            j0, n = widths[i]
-            nc.vector.quantize_mx(out=y_codes[:, j0 : j0 + n].bitcast(FP8X4), scales=y_scales[:, j0 : j0 + n], in_=y_bf[i][:])
+        def add_step(h, tp, a, b):
+            rows = slice(2 * tp, 2 * tp + 2)
+            base = sp[h][:, rows, a:b] if tp == 0 else c_bank[1][h][:, :, a:b]
+            nc.vector.scalar_tensor_tensor(y[h][:, rows, a:b], step[h][:, rows, a:b], 0.5, base, ALU.mult, ALU.add)
 
         def store_y(i):
-            j0, n = widths[i]
-            nc.sync.dma_start(out_rows[:, :, j0 : j0 + n], y[i][:])
+            h, a, b = pieces[i]
+            nc.sync.dma_start(out_rows[:, :, HALF * h + a : HALF * h + b], y[h][:, :, a:b])
+
+        def weave(copy, i):
+            h, a, b = pieces[i]
+            copy(y_bf[i][:].rearrange("p (c i t) -> p c t i", i=4, t=PACK), y[h][:, :, a:b].rearrange("p t (c i) -> p c t i", i=4))
+
+        def quant_y(i):
+            h, a, b = pieces[i]
+            cols = slice(HALF * h + a, HALF * h + b)
+            nc.vector.quantize_mx(out=y_codes[:, cols].bitcast(FP8X4), scales=y_scales[:, cols], in_=y_bf[i][:])
 
         for tp in range(2):
-            rows = slice(2 * tp, 2 * tp + 2)
-            nc.vector.tensor_tensor(step[0][:, rows, :], gate[0][:, rows, :], diff[(0, tp)], ALU.mult)
+            scale_step(0, tp)
         for tp in range(2):
-            rows = slice(2 * tp, 2 * tp + 2)
-            nc.vector.tensor_tensor(y[0][:, rows, :], step[0][:, rows, :], sp[0][:, rows, :], ALU.add)
+            add_step(0, tp, 0, HALF)
         store_y(0)
-        weave(nc.scalar.copy, 0)
+        weave(scalar_copy, 0)
+        for tp in range(2):
+            scale_step(1, tp)
+        add_step(1, 0, 0, HALF)
         for i in (1, 2):
-            cols = slice(QUARTER * (i - 1), QUARTER * i)
-            nc.vector.tensor_tensor(step[1][:, :, cols], gate[1][:, :, cols], diff_rest[:, 2:6, cols], ALU.mult)
-        for i in (1, 2):
-            cols = slice(QUARTER * (i - 1), QUARTER * i)
-            nc.vector.tensor_tensor(y[i][:], step[1][:, :, cols], sp[1][:, :, cols], ALU.add)
+            add_step(1, 1, pieces[i][1], pieces[i][2])
             store_y(i)
-        weave(nc.scalar.copy, 1)
+        weave(scalar_copy, 1)
         quant_y(0)
         nc.sync.dma_start(out_words[:, 0:HALF], y_codes[:, 0:HALF].bitcast(I32))
         weave(nc.vector.tensor_copy, 2)

@@ -19,6 +19,7 @@ P = 128
 PACK = 4
 HALF = S // 2
 QUARTER = S // 4
+SCALAR_DEALT = 44
 
 
 def tile_picked_mingru8_none_po_kernel(tc, x_words, x_scales, w1, w2, st, offs, par, out_0, out_1, out_2):
@@ -68,9 +69,9 @@ def tile_picked_mingru8_none_po_kernel(tc, x_words, x_scales, w1, w2, st, offs, 
         w_codes = {}
         w_scales = [sb.tile([P, N], U8, name="w_scales%d" % w, align_bytes=64) for w in range(2)]
 
-        def deal(copy, w, h, a, b):
-            dst = w_bf[w][:].rearrange("p (t m j) -> p m j t", t=PACK, j=PACK)[:, 64 * h + a : 64 * h + b]
-            src = raw[w][h][:].rearrange("p j (m t) -> p m j t", t=PACK)[:, a:b]
+        def deal(copy, w, h, a, b, walk="p m j t"):
+            dst = w_bf[w][:].rearrange("p (t m j) -> " + walk, t=PACK, j=PACK)[:, 64 * h + a : 64 * h + b]
+            src = raw[w][h][:].rearrange("p j (m t) -> " + walk, t=PACK)[:, a:b]
             copy(dst, src)
 
         def quant_w(w, a, b, tag):
@@ -116,7 +117,8 @@ def tile_picked_mingru8_none_po_kernel(tc, x_words, x_scales, w1, w2, st, offs, 
         for h in range(2):
             nc.vector.tensor_tensor(diff[h][:, 2, :], sp[h][:, 2, :], c_bank[1][h][:, 0, :], ALU.subtract)
         deal(scalar_copy, 0, 0, 0, 64)
-        deal(scalar_copy, 0, 1, 0, 64)
+        deal(scalar_copy, 0, 1, 0, SCALAR_DEALT)
+        deal(nc.gpsimd.tensor_copy, 0, 1, SCALAR_DEALT, 64, "p m t j")
         quant_w(0, 0, 2, "codes00")
         quant_w(0, 2, 4, "codes01")
         c_last = sb.tile([P, 2, HALF], F32, name="c_last", tag="raw01", align_bytes=64)

@@ -114,8 +114,7 @@ def tile_picked_mingru8_none_po_kernel(tc, x_words, x_scales, w1, w2, st, offs, 
         diff = [sb.tile([P, PACK, HALF], F32, name="diff%d" % h, align_bytes=64) for h in range(2)]
         for h in range(2):
             nc.vector.tensor_tensor(diff[h][:, 0:2, :], c_bank[0][h][:], sp[h][:, 0:2, :], ALU.subtract)
-        for h in range(2):
-            nc.vector.tensor_tensor(diff[h][:, 2, :], sp[h][:, 2, :], c_bank[1][h][:, 0, :], ALU.subtract)
+        nc.vector.tensor_tensor(diff[0][:, 2, :], sp[0][:, 2, :], c_bank[1][0][:, 0, :], ALU.subtract)
         deal(scalar_copy, 0, 0, 0, 64)
         deal(scalar_copy, 0, 1, 0, SCALAR_DEALT)
         deal(nc.gpsimd.tensor_copy, 0, 1, SCALAR_DEALT, 64, "p m t j")
@@ -125,6 +124,7 @@ def tile_picked_mingru8_none_po_kernel(tc, x_words, x_scales, w1, w2, st, offs, 
         for h in range(2):
             scalar_copy(c_last[:, h, :], c_bank[1][h][:, 1, :])
             nc.vector.tensor_tensor(diff[h][:, 3, :], st_t[3][:].indirect(par_t[:, 16 * h : 16 * (h + 1)]), c_last[:, h, :], ALU.subtract)
+        nc.vector.tensor_tensor(diff[1][:, 2, :], sp[1][:, 2, :], c_bank[1][1][:, 0, :], ALU.subtract)
 
         gate = [sb.tile([P, PACK, HALF], F32, name="gate%d" % h, align_bytes=64) for h in range(2)]
         step = [sb.tile([P, PACK, HALF], F32, name="step%d" % h, align_bytes=64) for h in range(2)]

@@ -179,11 +179,11 @@ def tile_picked_mingru8_none_po_kernel(tc, x_words, x_scales, w1, w2, st, offs, 
             store_y(i)
         weave(scalar_copy, 1)
         quant_y(0)
-        nc.sync.dma_start(out_words[:, 0:HALF], y_codes[:, 0:HALF].bitcast(I32))
+        nc.scalar.dma_start(out_words[:, 0:HALF], y_codes[:, 0:HALF].bitcast(I32))
         weave(nc.vector.tensor_copy, 2)
         quant_y(1)
         quant_y(2)
-        nc.sync.dma_start(out_words[:, HALF:S], y_codes[:, HALF:S].bitcast(I32))
+        nc.scalar.dma_start(out_words[:, HALF:S], y_codes[:, HALF:S].bitcast(I32))
         for q in range(4):
-            queue = nc.scalar if q % 2 == 0 else nc.sync
+            queue = nc.scalar if q == 0 else nc.sync
             queue.dma_start(out_2[0, 4 * q : 4 * q + 4, :].bitcast(I32), y_scales[32 * q : 32 * q + 4, :].bitcast(I32))

@@ -173,9 +173,9 @@ def tile_picked_mingru8_none_po_kernel(tc, x_words, x_scales, w1, w2, st, offs, 
         weave(scalar_copy, 0)
         for tp in range(2):
             scale_step(1, tp)
-        add_step(1, 0, 0, HALF)
         for i in (1, 2):
-            add_step(1, 1, pieces[i][1], pieces[i][2])
+            for tp in range(2):
+                add_step(1, tp, pieces[i][1], pieces[i][2])
             store_y(i)
         weave(scalar_copy, 1)
         quant_y(0)

@@ -59,13 +59,18 @@ def tile_picked_mingru8_none_po_kernel(tc, x_words, x_scales, w1, w2, st, offs, 
         load_w(0, 1)
         nc.sync.dma_start(st_t[3][:], st_rows[:, 3, :])
 
-        sp = [sb.tile([P, PACK - 1, HALF], F32, name="sp%d" % h, align_bytes=64) for h in range(2)]
+        warm_in = sb.tile([P, 1], F32, name="warm_in")
+        warm_out = sb.tile([P, 1], F32, name="warm_out")
+        nc.gpsimd.memset(warm_in[:], 0.0)
+        nc.scalar.activation(warm_out[:], warm_in[:], ACT.Sigmoid)
+
+        base = [sb.tile([P, PACK, HALF], F32, name="base%d" % h, align_bytes=64) for h in range(2)]
 
         def gather_state(t):
             for h in range(2):
-                nc.vector.tensor_copy(sp[h][:, t, :], st_t[t][:].indirect(par_t[:, 16 * h : 16 * (h + 1)]))
+                nc.vector.tensor_copy(base[h][:, t, :], st_t[t][:].indirect(par_t[:, 16 * h : 16 * (h + 1)]))
 
-        w_bf = [sb.tile([P, PACK * N], BF16, name="w_bf%d" % w, tag="w_bf%d" % w, align_bytes=64) for w in range(2)]
+        w_bf = [sb.tile([P, PACK * N], BF16, name="w_bf%d" % w, align_bytes=64) for w in range(2)]
         w_codes = {}
         w_scales = [sb.tile([P, N], U8, name="w_scales%d" % w, align_bytes=64) for w in range(2)]
 
@@ -74,8 +79,8 @@ def tile_picked_mingru8_none_po_kernel(tc, x_words, x_scales, w1, w2, st, offs, 
             src = raw[w][h][:].rearrange("p j (m t) -> " + walk, t=PACK)[:, a:b]
             copy(dst, src)
 
-        def quant_w(w, a, b, tag):
-            codes = sb.tile([P, P * (b - a)], U32, name="w_codes%d%d" % (w, a), tag=tag, align_bytes=64)
+        def quant_w(w, a, b):
+            codes = sb.tile([P, P * (b - a)], U32, name="w_codes%d%d" % (w, a), align_bytes=64)
             nc.vector.quantize_mx(out=codes[:].bitcast(FP8X4), scales=w_scales[w][:, P * a : P * b], in_=w_bf[w][:, PACK * P * a : PACK * P * b])
             for t in range(a, b):
                 w_codes[(w, t)] = codes[:, P * (t - a) : P * (t - a + 1)]
@@ -83,9 +88,9 @@ def tile_picked_mingru8_none_po_kernel(tc, x_words, x_scales, w1, w2, st, offs, 
         xg_w = [sb.tile([P, HALF], U32, name="xg_w%d" % h, align_bytes=64) for h in range(2)]
         xg_s = sb.tile([P, S], U8, name="xg_s", align_bytes=64)
 
-        def product(bank, w, h, t):
+        def product(out, w, h, t):
             nc.tensor.matmul_mx(
-                out=bank[:, t % 2, :],
+                out=out,
                 lhsT=w_codes[(w, t)].bitcast(FP8X4),
                 lhsT_scale=w_scales[w][:, P * t : P * (t + 1)],
                 rhs=xg_w[h][:].bitcast(FP8X4),
@@ -94,63 +99,59 @@ def tile_picked_mingru8_none_po_kernel(tc, x_words, x_scales, w1, w2, st, offs, 
                 stop=True,
             )
 
-        def scalar_copy(dst, src):
-            nc.scalar.activation(dst, src, ACT.Copy)
-
         for t in range(3):
             gather_state(t)
         nc.vector.tensor_copy(xg_s[:], x_s[:].indirect(offs_t[:]))
-        deal(scalar_copy, 1, 0, 0, 64)
-        deal(scalar_copy, 1, 1, 0, 64)
-        quant_w(1, 0, 4, "codes1")
+        deal(nc.scalar.copy, 1, 0, 0, 64)
+        deal(nc.scalar.copy, 1, 1, 0, 64)
+        quant_w(1, 0, 4)
         for h in range(2):
             nc.vector.tensor_copy(xg_w[h][:], x_w[:].indirect(offs_t[:, 16 * h : 16 * (h + 1)]))
-        c_bank = [[ps.tile([P, 2, HALF], F32, name="c_bank%d%d" % (tp, h)) for h in range(2)] for tp in range(2)]
-        for tp in range(2):
+        c_pair = [ps.tile([P, 2, HALF], F32, name="c_pair%d" % h) for h in range(2)]
+        c_plane = {t: ps.tile([P, 2, HALF], F32, name="c_plane%d" % t) for t in (2, 3)}
+        for h in range(2):
+            for t in range(2):
+                product(c_pair[h][:, t, :], 1, h, t)
+        for t in (2, 3):
             for h in range(2):
-                for t in (2 * tp, 2 * tp + 1):
-                    product(c_bank[tp][h], 1, h, t)
+                product(c_plane[t][:, h, :], 1, h, t)
 
         diff = [sb.tile([P, PACK, HALF], F32, name="diff%d" % h, align_bytes=64) for h in range(2)]
-        for h in range(2):
-            nc.vector.tensor_tensor(diff[h][:, 0:2, :], c_bank[0][h][:], sp[h][:, 0:2, :], ALU.subtract)
-        nc.vector.tensor_tensor(diff[0][:, 2, :], sp[0][:, 2, :], c_bank[1][0][:, 0, :], ALU.subtract)
-        deal(scalar_copy, 0, 0, 0, 64)
-        deal(scalar_copy, 0, 1, 0, SCALAR_DEALT)
+        nc.vector.tensor_tensor(diff[0][:, 0:2, :], base[0][:, 0:2, :], c_pair[0][:], ALU.subtract)
+        nc.vector.tensor_tensor(diff[1][:, 0:2, :], c_pair[1][:], base[1][:, 0:2, :], ALU.subtract)
+        nc.vector.tensor_tensor(diff[0][:, 2, :], base[0][:, 2, :], c_plane[2][:, 0, :], ALU.subtract)
+        nc.vector.tensor_tensor(diff[1][:, 2, :], c_plane[2][:, 1, :], base[1][:, 2, :], ALU.subtract)
+        deal(nc.scalar.copy, 0, 0, 0, 64)
+        deal(nc.scalar.copy, 0, 1, 0, SCALAR_DEALT)
         deal(nc.gpsimd.tensor_copy, 0, 1, SCALAR_DEALT, 64, "p m t j")
-        quant_w(0, 0, 2, "codes00")
-        quant_w(0, 2, 4, "codes01")
-        c_last = sb.tile([P, 2, HALF], F32, name="c_last", tag="raw01", align_bytes=64)
+        quant_w(0, 0, 2)
+        quant_w(0, 2, 4)
+        c_first = sb.tile([P, HALF], F32, name="c_first", tag="raw01", align_bytes=64)
+        c_last = [c_first[:], base[1][:, 3, :]]
         for h in range(2):
-            scalar_copy(c_last[:, h, :], c_bank[1][h][:, 1, :])
-            nc.vector.tensor_tensor(diff[h][:, 3, :], st_t[3][:].indirect(par_t[:, 16 * h : 16 * (h + 1)]), c_last[:, h, :], ALU.subtract)
-        nc.vector.tensor_tensor(diff[1][:, 2, :], sp[1][:, 2, :], c_bank[1][1][:, 0, :], ALU.subtract)
+            nc.scalar.copy(c_last[h], c_plane[3][:, h, :])
+            nc.vector.tensor_tensor(diff[h][:, 3, :], st_t[3][:].indirect(par_t[:, 16 * h : 16 * (h + 1)]), c_last[h], ALU.subtract)
 
-        gate = [sb.tile([P, PACK, HALF], F32, name="gate%d" % h, align_bytes=64) for h in range(2)]
-        step = [sb.tile([P, PACK, HALF], F32, name="step%d" % h, align_bytes=64) for h in range(2)]
+        gate = {}
         for h in range(2):
             for tp in range(2):
-                u_bank = ps.tile([P, 2, HALF], F32, name="u_bank%d%d" % (tp, h))
-                for t in (2 * tp, 2 * tp + 1):
-                    product(u_bank, 0, h, t)
-                nc.scalar.activation(gate[h][:, 2 * tp : 2 * tp + 2, :], u_bank[:], ACT.Tanh, scale=0.5 if tp == 0 else -0.5)
+                u_bank = ps.tile([P, 2, HALF], F32, name="u_bank%d%d" % (h, tp))
+                for i in range(2):
+                    product(u_bank[:, i, :], 0, h, 2 * tp + i)
+                gate[(h, tp)] = sb.tile([P, 2, HALF], F32, name="gate%d%d" % (h, tp), tag="gate%d%d" % (h, tp), align_bytes=64)
+                if (h, tp) == (1, 1):
+                    nc.scalar.activation(gate[(h, tp)][:, 0, :], u_bank[:, 0, :], ACT.Sigmoid)
+                    nc.scalar.activation(gate[(h, tp)][:, 1, :], u_bank[:, 1, :], ACT.Sigmoid, scale=-1.0)
+                else:
+                    nc.scalar.activation(gate[(h, tp)][:], u_bank[:], ACT.Sigmoid, scale=-1.0 if h == 0 else 1.0)
 
-        y_codes = sb.tile([P, S], U32, name="y_codes", align_bytes=64)
         y_scales = sb.tile([P, S], U8, name="y_scales", align_bytes=64)
         out_rows = out_0.rearrange("(p t) j -> p t j", t=PACK)
         out_words = out_1[0].rearrange("p n r -> p (n r)").bitcast(I32)
         y = [sb.tile([P, PACK, HALF], F32, name="y%d" % h, align_bytes=64) for h in range(2)]
+        step = [sb.tile([P, PACK, HALF], F32, name="step%d" % h, tag=("step0", "gate00")[h], align_bytes=64) for h in range(2)]
         pieces = [(0, 0, HALF), (1, 0, QUARTER), (1, QUARTER, HALF)]
         y_bf = [sb.tile([P, PACK * (b - a)], BF16, name="y_bf%d" % i, align_bytes=64) for i, (h, a, b) in enumerate(pieces)]
-
-        def scale_step(h, tp):
-            rows = slice(2 * tp, 2 * tp + 2)
-            nc.vector.scalar_tensor_tensor(step[h][:, rows, :], gate[h][:, rows, :], 1.0, diff[h][:, rows, :], ALU.add, ALU.mult)
-
-        def add_step(h, tp, a, b):
-            rows = slice(2 * tp, 2 * tp + 2)
-            base = sp[h][:, rows, a:b] if tp == 0 else c_bank[1][h][:, :, a:b]
-            nc.vector.scalar_tensor_tensor(y[h][:, rows, a:b], step[h][:, rows, a:b], 0.5, base, ALU.mult, ALU.add)
 
         def store_y(i):
             h, a, b = pieces[i]
@@ -163,27 +164,32 @@ def tile_picked_mingru8_none_po_kernel(tc, x_words, x_scales, w1, w2, st, offs, 
         def quant_y(i):
             h, a, b = pieces[i]
             cols = slice(HALF * h + a, HALF * h + b)
-            nc.vector.quantize_mx(out=y_codes[:, cols].bitcast(FP8X4), scales=y_scales[:, cols], in_=y_bf[i][:])
+            nc.vector.quantize_mx(out=y_codes[h][:, a:b].bitcast(FP8X4), scales=y_scales[:, cols], in_=y_bf[i][:])
 
         for tp in range(2):
-            scale_step(0, tp)
-        for tp in range(2):
-            add_step(0, tp, 0, HALF)
+            rows = slice(2 * tp, 2 * tp + 2)
+            nc.vector.tensor_tensor(step[0][:, rows, :], gate[(0, tp)][:], diff[0][:, rows, :], ALU.mult)
+        nc.gpsimd.tensor_tensor(step[1][:, 0:2, :], gate[(1, 0)][:], diff[1][:, 0:2, :], ALU.mult)
+        nc.vector.tensor_tensor(y[0][:, 0:2, :], step[0][:, 0:2, :], c_pair[0][:], ALU.add)
+        for t in (2, 3):
+            nc.vector.tensor_tensor(y[0][:, t, :], step[0][:, t, :], c_plane[t][:, 0, :], ALU.add)
         store_y(0)
-        weave(scalar_copy, 0)
-        for tp in range(2):
-            scale_step(1, tp)
+        weave(nc.scalar.copy, 0)
         for i in (1, 2):
-            for tp in range(2):
-                add_step(1, tp, pieces[i][1], pieces[i][2])
+            h, a, b = pieces[i]
+            nc.vector.tensor_tensor(step[1][:, 2:4, a:b], gate[(1, 1)][:, :, a:b], diff[1][:, 2:4, a:b], ALU.mult)
+        for i in (1, 2):
+            h, a, b = pieces[i]
+            nc.vector.tensor_tensor(y[1][:, :, a:b], step[1][:, :, a:b], base[1][:, :, a:b], ALU.add)
             store_y(i)
-        weave(scalar_copy, 1)
+        weave(nc.scalar.copy, 1)
+        y_codes = [sb.tile([P, HALF], U32, name="y_codes%d" % h, tag=("gate00", "y_codes1")[h], align_bytes=64) for h in range(2)]
         quant_y(0)
-        nc.scalar.dma_start(out_words[:, 0:HALF], y_codes[:, 0:HALF].bitcast(I32))
+        nc.scalar.dma_start(out_words[:, 0:HALF], y_codes[0][:].bitcast(I32))
         weave(nc.vector.tensor_copy, 2)
         quant_y(1)
         quant_y(2)
-        nc.scalar.dma_start(out_words[:, HALF:S], y_codes[:, HALF:S].bitcast(I32))
+        nc.scalar.dma_start(out_words[:, HALF:S], y_codes[1][:].bitcast(I32))
         for q in range(4):
             queue = nc.scalar if q == 0 else nc.sync
             queue.dma_start(out_2[0, 4 * q : 4 * q + 4, :].bitcast(I32), y_scales[32 * q : 32 * q + 4, :].bitcast(I32))

@@ -183,7 +183,7 @@ def tile_picked_mingru8_none_po_kernel(tc, x_words, x_scales, w1, w2, st, offs, 
             nc.vector.tensor_tensor(y[1][:, :, a:b], step[1][:, :, a:b], base[1][:, :, a:b], ALU.add)
             store_y(i)
         weave(nc.scalar.copy, 1)
-        y_codes = [sb.tile([P, HALF], U32, name="y_codes%d" % h, tag=("gate00", "y_codes1")[h], align_bytes=64) for h in range(2)]
+        y_codes = [sb.tile([P, HALF], U32, name="y_codes%d" % h, tag=("gate10", "y_codes1")[h], align_bytes=64) for h in range(2)]
         quant_y(0)
         nc.scalar.dma_start(out_words[:, 0:HALF], y_codes[0][:].bitcast(I32))
         weave(nc.vector.tensor_copy, 2)

@@ -61,7 +61,7 @@ def tile_picked_mingru8_none_po_kernel(tc, x_words, x_scales, w1, w2, st, offs, 
 
         warm_in = sb.tile([P, 1], F32, name="warm_in")
         warm_out = sb.tile([P, 1], F32, name="warm_out")
-        nc.gpsimd.memset(warm_in[:], 0.0)
+        nc.vector.memset(warm_in[:], 0.0)
         nc.scalar.activation(warm_out[:], warm_in[:], ACT.Sigmoid)
 
         base = [sb.tile([P, PACK, HALF], F32, name="base%d" % h, align_bytes=64) for h in range(2)]

@@ -19,7 +19,7 @@ P = 128
 PACK = 4
 HALF = S // 2
 QUARTER = S // 4
-SCALAR_DEALT = 44
+SCALAR_DEALT = 24
 
 
 def tile_picked_mingru8_none_po_kernel(tc, x_words, x_scales, w1, w2, st, offs, par, out_0, out_1, out_2):
@@ -32,129 +32,128 @@ def tile_picked_mingru8_none_po_kernel(tc, x_words, x_scales, w1, w2, st, offs, 
         offs_t = sb.tile([P, S // 16], U16, name="offs_t")
         x_w = sb.tile([P, T], U32, name="x_w", align_bytes=64)
         x_s = sb.tile([P, T], U8, name="x_s", align_bytes=64)
-        st_t = [sb.tile([P, S], F32, name="st%d" % t, align_bytes=64) for t in range(PACK)]
-        raw = [[sb.tile([P, PACK, HALF], F32, name="raw%d%d" % (w, h), tag="raw%d%d" % (w, h), align_bytes=64) for h in range(2)] for w in range(2)]
+        st_t = [sb.tile([P, S], F32, name="st%d" % t, tag="st%d" % t, align_bytes=64) for t in range(PACK)]
+        raw = [[sb.tile([P, PACK, HALF], F32, name="raw%d%d" % (w, h), align_bytes=64) for h in range(2)] for w in range(2)]
         st_rows = st.rearrange("(p t) j -> p t j", t=PACK)
         w_rows = [w.rearrange("(p j) m -> p j m", j=PACK) for w in (w1, w2)]
 
         def load_w(w, h):
             nc.sync.dma_start(raw[w][h][:], w_rows[w][:, :, h * HALF : (h + 1) * HALF])
 
-        def load_xs(q):
-            nc.sync.dma_start(x_s[32 * q : 32 * q + 4, :].bitcast(I32), x_scales[0, 4 * q : 4 * q + 4, :].bitcast(I32))
-
         nc.vector.memset(x_s[:].bitcast(I32), 0)
 
-        nc.sync.dma_start(st_t[0][:], st_rows[:, 0, :])
-        nc.sync.dma_start(par_t[:], par)
-        for t in (1, 2):
-            nc.sync.dma_start(st_t[t][:], st_rows[:, t, :])
-        load_w(1, 0)
+        load_w(0, 0)
         nc.sync.dma_start(offs_t[:], offs)
         for q in range(4):
-            load_xs(q)
-        load_w(1, 1)
-        nc.sync.dma_start(x_w[:].bitcast(I32), x_words[0].rearrange("p n r -> p (n r)").bitcast(I32))
-        load_w(0, 0)
+            nc.sync.dma_start(x_s[32 * q : 32 * q + 4, :].bitcast(I32), x_scales[0, 4 * q : 4 * q + 4, :].bitcast(I32))
         load_w(0, 1)
-        nc.sync.dma_start(st_t[3][:], st_rows[:, 3, :])
+        nc.sync.dma_start(x_w[:].bitcast(I32), x_words[0].rearrange("p n r -> p (n r)").bitcast(I32))
+        load_w(1, 0)
+        load_w(1, 1)
+        nc.sync.dma_start(par_t[:], par)
+        for t in range(PACK):
+            nc.sync.dma_start(st_t[t][:], st_rows[:, t, :])
 
         warm_in = sb.tile([P, 1], F32, name="warm_in")
         warm_out = sb.tile([P, 1], F32, name="warm_out")
         nc.vector.memset(warm_in[:], 0.0)
         nc.scalar.activation(warm_out[:], warm_in[:], ACT.Sigmoid)
 
-        base = [sb.tile([P, PACK, HALF], F32, name="base%d" % h, align_bytes=64) for h in range(2)]
-
-        def gather_state(t):
-            for h in range(2):
-                nc.vector.tensor_copy(base[h][:, t, :], st_t[t][:].indirect(par_t[:, 16 * h : 16 * (h + 1)]))
-
         w_bf = [sb.tile([P, PACK * N], BF16, name="w_bf%d" % w, align_bytes=64) for w in range(2)]
-        w_codes = {}
+        w_codes = [sb.tile([P, N], U32, name="w_codes%d" % w, align_bytes=64) for w in range(2)]
         w_scales = [sb.tile([P, N], U8, name="w_scales%d" % w, align_bytes=64) for w in range(2)]
 
-        def deal(copy, w, h, a, b, walk="p m j t"):
-            dst = w_bf[w][:].rearrange("p (t m j) -> " + walk, t=PACK, j=PACK)[:, 64 * h + a : 64 * h + b]
-            src = raw[w][h][:].rearrange("p j (m t) -> " + walk, t=PACK)[:, a:b]
+        def deal(copy, w, h, a, b, t0=0, t1=PACK):
+            dst = w_bf[w][:].rearrange("p (t m j) -> p m j t", t=PACK, j=PACK)[:, 64 * h + a : 64 * h + b, :, t0:t1]
+            src = raw[w][h][:].rearrange("p j (m t) -> p m j t", t=PACK)[:, a:b, :, t0:t1]
             copy(dst, src)
 
-        def quant_w(w, a, b):
-            codes = sb.tile([P, P * (b - a)], U32, name="w_codes%d%d" % (w, a), align_bytes=64)
-            nc.vector.quantize_mx(out=codes[:].bitcast(FP8X4), scales=w_scales[w][:, P * a : P * b], in_=w_bf[w][:, PACK * P * a : PACK * P * b])
-            for t in range(a, b):
-                w_codes[(w, t)] = codes[:, P * (t - a) : P * (t - a + 1)]
+        def quant_w(w, t0=0, t1=PACK):
+            cols = slice(P * t0, P * t1)
+            nc.vector.quantize_mx(out=w_codes[w][:, cols].bitcast(FP8X4), scales=w_scales[w][:, cols], in_=w_bf[w][:, PACK * P * t0 : PACK * P * t1])
 
         xg_w = [sb.tile([P, HALF], U32, name="xg_w%d" % h, align_bytes=64) for h in range(2)]
         xg_s = sb.tile([P, S], U8, name="xg_s", align_bytes=64)
 
-        def product(out, w, h, t):
-            nc.tensor.matmul_mx(
-                out=out,
-                lhsT=w_codes[(w, t)].bitcast(FP8X4),
-                lhsT_scale=w_scales[w][:, P * t : P * (t + 1)],
-                rhs=xg_w[h][:].bitcast(FP8X4),
-                rhs_scale=xg_s[:, HALF * h : HALF * (h + 1)],
-                start=True,
-                stop=True,
-            )
+        def products(w, h, tp):
+            bank = ps.tile([P, 2, HALF], F32, name="bank%d%d%d" % (w, h, tp))
+            for i in range(2):
+                cols = slice(P * (2 * tp + i), P * (2 * tp + i + 1))
+                nc.tensor.matmul_mx(
+                    out=bank[:, i, :],
+                    lhsT=w_codes[w][:, cols].bitcast(FP8X4),
+                    lhsT_scale=w_scales[w][:, cols],
+                    rhs=xg_w[h][:].bitcast(FP8X4),
+                    rhs_scale=xg_s[:, HALF * h : HALF * (h + 1)],
+                    start=True,
+                    stop=True,
+                )
+            return bank
 
-        for t in range(3):
-            gather_state(t)
+        def listed(t, h):
+            return st_t[t][:].indirect(par_t[:, 16 * h : 16 * (h + 1)])
+
+        deal(nc.vector.tensor_copy, 0, 0, 0, 64)
         nc.vector.tensor_copy(xg_s[:], x_s[:].indirect(offs_t[:]))
-        deal(nc.scalar.copy, 1, 0, 0, 64)
-        deal(nc.scalar.copy, 1, 1, 0, 64)
-        quant_w(1, 0, 4)
+        deal(nc.scalar.copy, 0, 1, 0, SCALAR_DEALT)
+        deal(nc.vector.tensor_copy, 0, 1, SCALAR_DEALT, 64)
+        quant_w(0)
         for h in range(2):
             nc.vector.tensor_copy(xg_w[h][:], x_w[:].indirect(offs_t[:, 16 * h : 16 * (h + 1)]))
-        c_pair = [ps.tile([P, 2, HALF], F32, name="c_pair%d" % h) for h in range(2)]
-        c_plane = {t: ps.tile([P, 2, HALF], F32, name="c_plane%d" % t) for t in (2, 3)}
-        for h in range(2):
-            for t in range(2):
-                product(c_pair[h][:, t, :], 1, h, t)
-        for t in (2, 3):
-            for h in range(2):
-                product(c_plane[t][:, h, :], 1, h, t)
 
-        diff = [sb.tile([P, PACK, HALF], F32, name="diff%d" % h, align_bytes=64) for h in range(2)]
-        nc.vector.tensor_tensor(diff[0][:, 0:2, :], base[0][:, 0:2, :], c_pair[0][:], ALU.subtract)
-        nc.vector.tensor_tensor(diff[1][:, 0:2, :], c_pair[1][:], base[1][:, 0:2, :], ALU.subtract)
-        nc.vector.tensor_tensor(diff[0][:, 2, :], base[0][:, 2, :], c_plane[2][:, 0, :], ALU.subtract)
-        nc.vector.tensor_tensor(diff[1][:, 2, :], c_plane[2][:, 1, :], base[1][:, 2, :], ALU.subtract)
-        deal(nc.scalar.copy, 0, 0, 0, 64)
-        deal(nc.scalar.copy, 0, 1, 0, SCALAR_DEALT)
-        deal(nc.gpsimd.tensor_copy, 0, 1, SCALAR_DEALT, 64, "p m t j")
-        quant_w(0, 0, 2)
-        quant_w(0, 2, 4)
-        c_first = sb.tile([P, HALF], F32, name="c_first", tag="raw01", align_bytes=64)
-        c_last = [c_first[:], base[1][:, 3, :]]
-        for h in range(2):
-            nc.scalar.copy(c_last[h], c_plane[3][:, h, :])
-            nc.vector.tensor_tensor(diff[h][:, 3, :], st_t[3][:].indirect(par_t[:, 16 * h : 16 * (h + 1)]), c_last[h], ALU.subtract)
+        units = [(h, tp) for h in range(2) for tp in range(2)]
+        u_bank = {(h, tp): products(0, h, tp) for tp in range(2) for h in range(2)}
+        gate = {u: sb.tile([P, 2, HALF], F32, name="gate%d%d" % u, tag="gate%d%d" % u, align_bytes=64) for u in units}
 
-        gate = {}
-        for h in range(2):
-            for tp in range(2):
-                u_bank = ps.tile([P, 2, HALF], F32, name="u_bank%d%d" % (h, tp))
-                for i in range(2):
-                    product(u_bank[:, i, :], 0, h, 2 * tp + i)
-                gate[(h, tp)] = sb.tile([P, 2, HALF], F32, name="gate%d%d" % (h, tp), tag="gate%d%d" % (h, tp), align_bytes=64)
-                if (h, tp) == (1, 1):
-                    nc.scalar.activation(gate[(h, tp)][:, 0, :], u_bank[:, 0, :], ACT.Sigmoid)
-                    nc.scalar.activation(gate[(h, tp)][:, 1, :], u_bank[:, 1, :], ACT.Sigmoid, scale=-1.0)
-                else:
-                    nc.scalar.activation(gate[(h, tp)][:], u_bank[:], ACT.Sigmoid, scale=-1.0 if h == 0 else 1.0)
+        def make_gate(u):
+            nc.scalar.activation(gate[u][:], u_bank[u][:], ACT.Sigmoid, scale=-1.0)
+
+        def gather_states(dst, u):
+            h, tp = u
+            for i in range(2):
+                nc.scalar.activation(dst[:, i, :], listed(2 * tp + i, h), ACT.Copy)
+
+        base10 = sb.tile([P, 2, HALF], F32, name="base10", align_bytes=64)
+        base11 = sb.tile([P, 2, HALF], F32, name="base11", align_bytes=64)
+        make_gate((0, 0))
+        make_gate((1, 0))
+        gather_states(base10, (1, 0))
+        make_gate((0, 1))
+        make_gate((1, 1))
+
+        keep0 = sb.tile([P, PACK, HALF], F32, name="keep0", align_bytes=64)
+        deal(nc.vector.tensor_copy, 1, 0, 0, 64)
+        for tp in range(2):
+            deal(nc.vector.tensor_copy, 1, 1, 0, 64, 2 * tp, 2 * tp + 2)
+        for tp in range(2):
+            quant_w(1, 2 * tp, 2 * tp + 2)
+        for t in range(2):
+            nc.vector.tensor_tensor(keep0[:, t, :], listed(t, 0), gate[(0, 0)][:, t, :], ALU.mult)
+        keep = [keep0, sb.tile([P, PACK, HALF], F32, name="keep1", tag="st1", align_bytes=64)]
+        base01 = keep[1][:, 2:4, :]
+        gather_states(base01, (0, 1))
+        gather_states(base11, (1, 1))
+        nc.gpsimd.tensor_tensor(keep[1][:, 0:2, :], gate[(1, 0)][:], base10[:], ALU.mult)
+        nc.gpsimd.tensor_tensor(keep[0][:, 2, :], gate[(0, 1)][:, 0, :], base01[:, 0, :], ALU.mult)
+
+        fresh = [sb.tile([P, PACK, HALF], F32, name="fresh%d" % h, align_bytes=64) for h in range(2)]
+        for u in units:
+            h, tp = u
+            c_bank = products(1, h, tp)
+            nc.vector.scalar_tensor_tensor(fresh[h][:, 2 * tp : 2 * tp + 2, :], gate[u][:], 1.0, c_bank[:], ALU.subtract, ALU.mult)
+        nc.vector.tensor_tensor(keep[0][:, 3, :], gate[(0, 1)][:, 1, :], base01[:, 1, :], ALU.mult)
 
         y_scales = sb.tile([P, S], U8, name="y_scales", align_bytes=64)
         out_rows = out_0.rearrange("(p t) j -> p t j", t=PACK)
         out_words = out_1[0].rearrange("p n r -> p (n r)").bitcast(I32)
         y = [sb.tile([P, PACK, HALF], F32, name="y%d" % h, align_bytes=64) for h in range(2)]
-        step = [sb.tile([P, PACK, HALF], F32, name="step%d" % h, tag=("step0", "gate00")[h], align_bytes=64) for h in range(2)]
         pieces = [(0, 0, HALF), (1, 0, QUARTER), (1, QUARTER, HALF)]
         y_bf = [sb.tile([P, PACK * (b - a)], BF16, name="y_bf%d" % i, align_bytes=64) for i, (h, a, b) in enumerate(pieces)]
+        y_codes = [sb.tile([P, HALF], U32, name="y_codes%d" % h, align_bytes=64) for h in range(2)]
 
-        def store_y(i):
+        def finish(i):
             h, a, b = pieces[i]
+            nc.vector.tensor_tensor(y[h][:, :, a:b], keep[h][:, :, a:b], fresh[h][:, :, a:b], ALU.subtract)
             nc.sync.dma_start(out_rows[:, :, HALF * h + a : HALF * h + b], y[h][:, :, a:b])
 
         def weave(copy, i):
@@ -166,24 +165,12 @@ def tile_picked_mingru8_none_po_kernel(tc, x_words, x_scales, w1, w2, st, offs, 
             cols = slice(HALF * h + a, HALF * h + b)
             nc.vector.quantize_mx(out=y_codes[h][:, a:b].bitcast(FP8X4), scales=y_scales[:, cols], in_=y_bf[i][:])
 
-        for tp in range(2):
-            rows = slice(2 * tp, 2 * tp + 2)
-            nc.vector.tensor_tensor(step[0][:, rows, :], gate[(0, tp)][:], diff[0][:, rows, :], ALU.mult)
-        nc.gpsimd.tensor_tensor(step[1][:, 0:2, :], gate[(1, 0)][:], diff[1][:, 0:2, :], ALU.mult)
-        nc.vector.tensor_tensor(y[0][:, 0:2, :], step[0][:, 0:2, :], c_pair[0][:], ALU.add)
-        for t in (2, 3):
-            nc.vector.tensor_tensor(y[0][:, t, :], step[0][:, t, :], c_plane[t][:, 0, :], ALU.add)
-        store_y(0)
+        finish(0)
         weave(nc.scalar.copy, 0)
-        for i in (1, 2):
-            h, a, b = pieces[i]
-            nc.vector.tensor_tensor(step[1][:, 2:4, a:b], gate[(1, 1)][:, :, a:b], diff[1][:, 2:4, a:b], ALU.mult)
-        for i in (1, 2):
-            h, a, b = pieces[i]
-            nc.vector.tensor_tensor(y[1][:, :, a:b], step[1][:, :, a:b], base[1][:, :, a:b], ALU.add)
-            store_y(i)
+        nc.vector.tensor_tensor(keep[1][:, 2:4, :], gate[(1, 1)][:], base11[:], ALU.mult)
+        finish(1)
+        finish(2)
         weave(nc.scalar.copy, 1)
-        y_codes = [sb.tile([P, HALF], U32, name="y_codes%d" % h, tag=("gate10", "y_codes1")[h], align_bytes=64) for h in range(2)]
         quant_y(0)
         nc.scalar.dma_start(out_words[:, 0:HALF], y_codes[0][:].bitcast(I32))
         weave(nc.vector.tensor_copy, 2)

@@ -33,12 +33,13 @@ def tile_picked_mingru8_none_po_kernel(tc, x_words, x_scales, w1, w2, st, offs, 
         x_w = sb.tile([P, T], U32, name="x_w", align_bytes=64)
         x_s = sb.tile([P, T], U8, name="x_s", align_bytes=64)
         st_t = [sb.tile([P, S], F32, name="st%d" % t, tag="st%d" % t, align_bytes=64) for t in range(PACK)]
-        raw = [[sb.tile([P, PACK, HALF], F32, name="raw%d%d" % (w, h), align_bytes=64) for h in range(2)] for w in range(2)]
+        w_cuts = [(0, HALF, N), (0, HALF, HALF + QUARTER, N)]
+        raw = [[sb.tile([P, PACK, b - a], F32, name="raw%d%d" % (w, a), align_bytes=64) for a, b in zip(cuts, cuts[1:])] for w, cuts in enumerate(w_cuts)]
         st_rows = st.rearrange("(p t) j -> p t j", t=PACK)
         w_rows = [w.rearrange("(p j) m -> p j m", j=PACK) for w in (w1, w2)]
 
         def load_w(w, h):
-            nc.sync.dma_start(raw[w][h][:], w_rows[w][:, :, h * HALF : (h + 1) * HALF])
+            nc.sync.dma_start(raw[w][h][:], w_rows[w][:, :, w_cuts[w][h] : w_cuts[w][h + 1]])
 
         nc.vector.memset(x_s[:].bitcast(I32), 0)
 
@@ -48,8 +49,8 @@ def tile_picked_mingru8_none_po_kernel(tc, x_words, x_scales, w1, w2, st, offs, 
             nc.sync.dma_start(x_s[32 * q : 32 * q + 4, :].bitcast(I32), x_scales[0, 4 * q : 4 * q + 4, :].bitcast(I32))
         load_w(0, 1)
         nc.sync.dma_start(x_w[:].bitcast(I32), x_words[0].rearrange("p n r -> p (n r)").bitcast(I32))
-        load_w(1, 0)
-        load_w(1, 1)
+        for h in range(3):
+            load_w(1, h)
         nc.sync.dma_start(par_t[:], par)
         for t in range(PACK):
             nc.sync.dma_start(st_t[t][:], st_rows[:, t, :])
@@ -64,7 +65,7 @@ def tile_picked_mingru8_none_po_kernel(tc, x_words, x_scales, w1, w2, st, offs, 
         w_scales = [sb.tile([P, N], U8, name="w_scales%d" % w, align_bytes=64) for w in range(2)]
 
         def deal(copy, w, h, a, b, t0=0, t1=PACK):
-            dst = w_bf[w][:].rearrange("p (t m j) -> p m j t", t=PACK, j=PACK)[:, 64 * h + a : 64 * h + b, :, t0:t1]
+            dst = w_bf[w][:].rearrange("p (t m j) -> p m j t", t=PACK, j=PACK)[:, w_cuts[w][h] // PACK + a : w_cuts[w][h] // PACK + b, :, t0:t1]
             src = raw[w][h][:].rearrange("p j (m t) -> p m j t", t=PACK)[:, a:b, :, t0:t1]
             copy(dst, src)
 
@@ -102,46 +103,45 @@ def tile_picked_mingru8_none_po_kernel(tc, x_words, x_scales, w1, w2, st, offs, 
             nc.vector.tensor_copy(xg_w[h][:], x_w[:].indirect(offs_t[:, 16 * h : 16 * (h + 1)]))
 
         units = [(h, tp) for h in range(2) for tp in range(2)]
-        u_bank = {(h, tp): products(0, h, tp) for tp in range(2) for h in range(2)}
-        gate = {u: sb.tile([P, 2, HALF], F32, name="gate%d%d" % u, tag="gate%d%d" % u, align_bytes=64) for u in units}
+        u_bank = {u: products(0, *u) for u in units}
+        gate = sb.tile([P, PACK, S], F32, name="gate", align_bytes=64)
+        base = sb.tile([P, PACK, S], F32, name="base", align_bytes=64)
+        fresh = sb.tile([P, PACK, S], F32, name="fresh", align_bytes=64)
 
-        def make_gate(u):
-            nc.scalar.activation(gate[u][:], u_bank[u][:], ACT.Sigmoid, scale=-1.0)
-
-        def gather_states(dst, u):
+        def unit(tile, u):
             h, tp = u
-            for i in range(2):
-                nc.scalar.activation(dst[:, i, :], listed(2 * tp + i, h), ACT.Copy)
+            return tile[:, 2 * tp : 2 * tp + 2, HALF * h : HALF * (h + 1)]
 
-        base10 = sb.tile([P, 2, HALF], F32, name="base10", align_bytes=64)
-        base11 = sb.tile([P, 2, HALF], F32, name="base11", align_bytes=64)
-        make_gate((0, 0))
-        make_gate((1, 0))
-        gather_states(base10, (1, 0))
-        make_gate((0, 1))
-        make_gate((1, 1))
+        def run(tile, a, b):
+            return tile[:].rearrange("p t j -> p (t j)")[:, HALF * a : HALF * b]
 
-        keep0 = sb.tile([P, PACK, HALF], F32, name="keep0", align_bytes=64)
+        def gather_state(t, h):
+            nc.scalar.activation(base[:, t, HALF * h : HALF * (h + 1)], listed(t, h), ACT.Copy)
+
+        for u in units[:3]:
+            nc.scalar.activation(unit(gate, u), u_bank[u][:], ACT.Sigmoid, scale=-1.0)
+        for h in range(2):
+            gather_state(0, h)
+        gate_last = sb.tile([P, 2, HALF], F32, name="gate_last", tag="st0", align_bytes=64)
+        nc.scalar.activation(gate_last[:], u_bank[(1, 1)][:], ACT.Sigmoid, scale=-1.0)
+        for t, h in ((1, 1), (2, 0), (2, 1), (3, 1)):
+            gather_state(t, h)
+
         deal(nc.vector.tensor_copy, 1, 0, 0, 64)
+        deal(nc.vector.tensor_copy, 1, 1, 0, 32)
         for tp in range(2):
-            deal(nc.vector.tensor_copy, 1, 1, 0, 64, 2 * tp, 2 * tp + 2)
+            deal(nc.vector.tensor_copy, 1, 2, 0, 32, 2 * tp, 2 * tp + 2)
         for tp in range(2):
             quant_w(1, 2 * tp, 2 * tp + 2)
-        for t in range(2):
-            nc.vector.tensor_tensor(keep0[:, t, :], listed(t, 0), gate[(0, 0)][:, t, :], ALU.mult)
-        keep = [keep0, sb.tile([P, PACK, HALF], F32, name="keep1", tag="st1", align_bytes=64)]
-        base01 = keep[1][:, 2:4, :]
-        gather_states(base01, (0, 1))
-        gather_states(base11, (1, 1))
-        nc.gpsimd.tensor_tensor(keep[1][:, 0:2, :], gate[(1, 0)][:], base10[:], ALU.mult)
-        nc.gpsimd.tensor_tensor(keep[0][:, 2, :], gate[(0, 1)][:, 0, :], base01[:, 0, :], ALU.mult)
+        keep = sb.tile([P, PACK, S], F32, name="keep", align_bytes=64)
+        nc.vector.tensor_tensor(keep[:, 1, 0:HALF], listed(1, 0), gate[:, 1, 0:HALF], ALU.mult)
+        nc.gpsimd.tensor_tensor(keep[:, 0, :], gate[:, 0, :], base[:, 0, :], ALU.mult)
 
-        fresh = [sb.tile([P, PACK, HALF], F32, name="fresh%d" % h, align_bytes=64) for h in range(2)]
         for u in units:
-            h, tp = u
-            c_bank = products(1, h, tp)
-            nc.vector.scalar_tensor_tensor(fresh[h][:, 2 * tp : 2 * tp + 2, :], gate[u][:], 1.0, c_bank[:], ALU.subtract, ALU.mult)
-        nc.vector.tensor_tensor(keep[0][:, 3, :], gate[(0, 1)][:, 1, :], base01[:, 1, :], ALU.mult)
+            c_bank = products(1, *u)
+            nc.vector.scalar_tensor_tensor(unit(fresh, u), gate_last[:] if u == (1, 1) else unit(gate, u), 1.0, c_bank[:], ALU.subtract, ALU.mult)
+        nc.vector.tensor_tensor(keep[:, 3, 0:HALF], listed(3, 0), gate[:, 3, 0:HALF], ALU.mult)
+        nc.vector.tensor_tensor(run(keep, 3, 5), run(gate, 3, 5), run(base, 3, 5), ALU.mult)
 
         y_scales = sb.tile([P, S], U8, name="y_scales", align_bytes=64)
         out_rows = out_0.rearrange("(p t) j -> p t j", t=PACK)
@@ -151,10 +151,15 @@ def tile_picked_mingru8_none_po_kernel(tc, x_words, x_scales, w1, w2, st, offs, 
         y_bf = [sb.tile([P, PACK * (b - a)], BF16, name="y_bf%d" % i, align_bytes=64) for i, (h, a, b) in enumerate(pieces)]
         y_codes = [sb.tile([P, HALF], U32, name="y_codes%d" % h, align_bytes=64) for h in range(2)]
 
+        def store_y(i):
+            h, a, b = pieces[i]
+            nc.sync.dma_start(out_rows[:, :, HALF * h + a : HALF * h + b], y[h][:, :, a:b])
+
         def finish(i):
             h, a, b = pieces[i]
-            nc.vector.tensor_tensor(y[h][:, :, a:b], keep[h][:, :, a:b], fresh[h][:, :, a:b], ALU.subtract)
-            nc.sync.dma_start(out_rows[:, :, HALF * h + a : HALF * h + b], y[h][:, :, a:b])
+            cols = slice(HALF * h + a, HALF * h + b)
+            nc.vector.tensor_tensor(y[h][:, :, a:b], keep[:, :, cols], fresh[:, :, cols], ALU.subtract)
+            store_y(i)
 
         def weave(copy, i):
             h, a, b = pieces[i]
@@ -165,15 +170,18 @@ def tile_picked_mingru8_none_po_kernel(tc, x_words, x_scales, w1, w2, st, offs, 
             cols = slice(HALF * h + a, HALF * h + b)
             nc.vector.quantize_mx(out=y_codes[h][:, a:b].bitcast(FP8X4), scales=y_scales[:, cols], in_=y_bf[i][:])
 
-        finish(0)
+        for tp in range(2):
+            nc.vector.tensor_tensor(y[0][:, 2 * tp : 2 * tp + 2, :], unit(keep, (0, tp)), unit(fresh, (0, tp)), ALU.subtract)
+        store_y(0)
         weave(nc.scalar.copy, 0)
-        nc.vector.tensor_tensor(keep[1][:, 2:4, :], gate[(1, 1)][:], base11[:], ALU.mult)
-        finish(1)
-        finish(2)
-        weave(nc.scalar.copy, 1)
+        for h, a, b in pieces[1:]:
+            cols = slice(HALF + a, HALF + b)
+            nc.vector.tensor_tensor(keep[:, 2:4, cols], gate_last[:, :, a:b], base[:, 2:4, cols], ALU.mult)
+        for i in (1, 2):
+            finish(i)
+            weave(nc.scalar.copy, i)
         quant_y(0)
-        nc.scalar.dma_start(out_words[:, 0:HALF], y_codes[0][:].bitcast(I32))
-        weave(nc.vector.tensor_copy, 2)
+        nc.sync.dma_start(out_words[:, 0:HALF], y_codes[0][:].bitcast(I32))
         quant_y(1)
         quant_y(2)
         nc.scalar.dma_start(out_words[:, HALF:S], y_codes[1][:].bitcast(I32))

@@ -33,7 +33,7 @@ def tile_picked_mingru8_none_po_kernel(tc, x_words, x_scales, w1, w2, st, offs, 
         x_w = sb.tile([P, T], U32, name="x_w", align_bytes=64)
         x_s = sb.tile([P, T], U8, name="x_s", align_bytes=64)
         st_t = [sb.tile([P, S], F32, name="st%d" % t, tag="st%d" % t, align_bytes=64) for t in range(PACK)]
-        w_cuts = [(0, HALF, N), (0, HALF, HALF + QUARTER, N)]
+        w_cuts = [(0, HALF, N), (0, HALF, N)]
         raw = [[sb.tile([P, PACK, b - a], F32, name="raw%d%d" % (w, a), align_bytes=64) for a, b in zip(cuts, cuts[1:])] for w, cuts in enumerate(w_cuts)]
         st_rows = st.rearrange("(p t) j -> p t j", t=PACK)
         w_rows = [w.rearrange("(p j) m -> p j m", j=PACK) for w in (w1, w2)]
@@ -49,10 +49,10 @@ def tile_picked_mingru8_none_po_kernel(tc, x_words, x_scales, w1, w2, st, offs, 
             nc.sync.dma_start(x_s[32 * q : 32 * q + 4, :].bitcast(I32), x_scales[0, 4 * q : 4 * q + 4, :].bitcast(I32))
         load_w(0, 1)
         nc.sync.dma_start(x_w[:].bitcast(I32), x_words[0].rearrange("p n r -> p (n r)").bitcast(I32))
-        for h in range(3):
+        for h in range(2):
             load_w(1, h)
         nc.sync.dma_start(par_t[:], par)
-        for t in range(PACK):
+        for t in (1, 0, 2, 3):
             nc.sync.dma_start(st_t[t][:], st_rows[:, t, :])
 
         warm_in = sb.tile([P, 1], F32, name="warm_in")
@@ -112,9 +112,6 @@ def tile_picked_mingru8_none_po_kernel(tc, x_words, x_scales, w1, w2, st, offs, 
             h, tp = u
             return tile[:, 2 * tp : 2 * tp + 2, HALF * h : HALF * (h + 1)]
 
-        def run(tile, a, b):
-            return tile[:].rearrange("p t j -> p (t j)")[:, HALF * a : HALF * b]
-
         def gather_state(t, h):
             nc.scalar.activation(base[:, t, HALF * h : HALF * (h + 1)], listed(t, h), ACT.Copy)
 
@@ -124,64 +121,64 @@ def tile_picked_mingru8_none_po_kernel(tc, x_words, x_scales, w1, w2, st, offs, 
             gather_state(0, h)
         gate_last = sb.tile([P, 2, HALF], F32, name="gate_last", tag="st0", align_bytes=64)
         nc.scalar.activation(gate_last[:], u_bank[(1, 1)][:], ACT.Sigmoid, scale=-1.0)
-        for t, h in ((1, 1), (2, 0), (2, 1), (3, 1)):
-            gather_state(t, h)
+        for t in (2, 3):
+            for h in range(2):
+                gather_state(t, h)
 
         deal(nc.vector.tensor_copy, 1, 0, 0, 64)
-        deal(nc.vector.tensor_copy, 1, 1, 0, 32)
         for tp in range(2):
-            deal(nc.vector.tensor_copy, 1, 2, 0, 32, 2 * tp, 2 * tp + 2)
+            deal(nc.vector.tensor_copy, 1, 1, 0, 64, 2 * tp, 2 * tp + 2)
         for tp in range(2):
             quant_w(1, 2 * tp, 2 * tp + 2)
         keep = sb.tile([P, PACK, S], F32, name="keep", align_bytes=64)
-        nc.vector.tensor_tensor(keep[:, 1, 0:HALF], listed(1, 0), gate[:, 1, 0:HALF], ALU.mult)
-        nc.gpsimd.tensor_tensor(keep[:, 0, :], gate[:, 0, :], base[:, 0, :], ALU.mult)
+        for h in range(2):
+            cols = slice(HALF * h, HALF * (h + 1))
+            nc.vector.tensor_tensor(keep[:, 1, cols], listed(1, h), gate[:, 1, cols], ALU.mult)
+        keep0 = sb.tile([P, S], F32, name="keep0", tag="st1", align_bytes=64)
+        nc.gpsimd.tensor_tensor(keep0[:], gate[:, 0, :], base[:, 0, :], ALU.mult)
+        nc.gpsimd.tensor_tensor(keep[:, 2, 0:HALF], gate[:, 2, 0:HALF], base[:, 2, 0:HALF], ALU.mult)
 
         for u in units:
             c_bank = products(1, *u)
             nc.vector.scalar_tensor_tensor(unit(fresh, u), gate_last[:] if u == (1, 1) else unit(gate, u), 1.0, c_bank[:], ALU.subtract, ALU.mult)
-        nc.vector.tensor_tensor(keep[:, 3, 0:HALF], listed(3, 0), gate[:, 3, 0:HALF], ALU.mult)
-        nc.vector.tensor_tensor(run(keep, 3, 5), run(gate, 3, 5), run(base, 3, 5), ALU.mult)
 
         y_scales = sb.tile([P, S], U8, name="y_scales", align_bytes=64)
         out_rows = out_0.rearrange("(p t) j -> p t j", t=PACK)
         out_words = out_1[0].rearrange("p n r -> p (n r)").bitcast(I32)
-        y = [sb.tile([P, PACK, HALF], F32, name="y%d" % h, align_bytes=64) for h in range(2)]
+        y = sb.tile([P, PACK, S], F32, name="y", align_bytes=64)
         pieces = [(0, 0, HALF), (1, 0, QUARTER), (1, QUARTER, HALF)]
         y_bf = [sb.tile([P, PACK * (b - a)], BF16, name="y_bf%d" % i, align_bytes=64) for i, (h, a, b) in enumerate(pieces)]
         y_codes = [sb.tile([P, HALF], U32, name="y_codes%d" % h, align_bytes=64) for h in range(2)]
 
-        def store_y(i):
-            h, a, b = pieces[i]
-            nc.sync.dma_start(out_rows[:, :, HALF * h + a : HALF * h + b], y[h][:, :, a:b])
-
         def finish(i):
             h, a, b = pieces[i]
             cols = slice(HALF * h + a, HALF * h + b)
-            nc.vector.tensor_tensor(y[h][:, :, a:b], keep[:, :, cols], fresh[:, :, cols], ALU.subtract)
-            store_y(i)
+            nc.vector.tensor_tensor(y[:, 1:PACK, cols], keep[:, 1:PACK, cols], fresh[:, 1:PACK, cols], ALU.subtract)
+            nc.sync.dma_start(out_rows[:, :, cols], y[:, :, cols])
 
         def weave(copy, i):
             h, a, b = pieces[i]
-            copy(y_bf[i][:].rearrange("p (c i t) -> p c t i", i=4, t=PACK), y[h][:, :, a:b].rearrange("p t (c i) -> p c t i", i=4))
+            cols = slice(HALF * h + a, HALF * h + b)
+            copy(y_bf[i][:].rearrange("p (c i t) -> p c t i", i=4, t=PACK), y[:, :, cols].rearrange("p t (c i) -> p c t i", i=4))
 
         def quant_y(i):
             h, a, b = pieces[i]
             cols = slice(HALF * h + a, HALF * h + b)
             nc.vector.quantize_mx(out=y_codes[h][:, a:b].bitcast(FP8X4), scales=y_scales[:, cols], in_=y_bf[i][:])
 
-        for tp in range(2):
-            nc.vector.tensor_tensor(y[0][:, 2 * tp : 2 * tp + 2, :], unit(keep, (0, tp)), unit(fresh, (0, tp)), ALU.subtract)
-        store_y(0)
+        nc.vector.tensor_tensor(keep[:, 3, 0:HALF], gate[:, 3, 0:HALF], base[:, 3, 0:HALF], ALU.mult)
+        nc.vector.tensor_tensor(y[:, 0, :], keep0[:], fresh[:, 0, :], ALU.subtract)
+        finish(0)
         weave(nc.scalar.copy, 0)
         for h, a, b in pieces[1:]:
             cols = slice(HALF + a, HALF + b)
             nc.vector.tensor_tensor(keep[:, 2:4, cols], gate_last[:, :, a:b], base[:, 2:4, cols], ALU.mult)
-        for i in (1, 2):
-            finish(i)
-            weave(nc.scalar.copy, i)
+        finish(1)
+        finish(2)
+        weave(nc.scalar.copy, 1)
         quant_y(0)
-        nc.sync.dma_start(out_words[:, 0:HALF], y_codes[0][:].bitcast(I32))
+        nc.scalar.dma_start(out_words[:, 0:HALF], y_codes[0][:].bitcast(I32))
+        weave(nc.vector.tensor_copy, 2)
         quant_y(1)
         quant_y(2)
         nc.scalar.dma_start(out_words[:, HALF:S], y_codes[1][:].bitcast(I32))

@@ -104,48 +104,50 @@ def tile_picked_mingru8_none_po_kernel(tc, x_words, x_scales, w1, w2, st, offs, 
 
         units = [(h, tp) for h in range(2) for tp in range(2)]
         u_bank = {u: products(0, *u) for u in units}
-        gate = sb.tile([P, PACK, S], F32, name="gate", align_bytes=64)
-        base = sb.tile([P, PACK, S], F32, name="base", align_bytes=64)
+        gate01 = sb.tile([P, 2, S], F32, name="gate01", align_bytes=64)
+        base0 = sb.tile([P, S], F32, name="base0", align_bytes=64)
+        base3 = sb.tile([P, HALF], F32, name="base3", align_bytes=64)
+        keep = sb.tile([P, PACK, S], F32, name="keep", align_bytes=64)
         fresh = sb.tile([P, PACK, S], F32, name="fresh", align_bytes=64)
+        y = sb.tile([P, PACK, S], F32, name="y", align_bytes=64)
+        base2 = y[:, 0, 0:HALF]
+        gate = {(0, 0): gate01[:, :, 0:HALF], (1, 0): gate01[:, :, HALF:S], (0, 1): keep[:, 2:4, HALF:S]}
 
         def unit(tile, u):
             h, tp = u
             return tile[:, 2 * tp : 2 * tp + 2, HALF * h : HALF * (h + 1)]
 
-        def gather_state(t, h):
-            nc.scalar.activation(base[:, t, HALF * h : HALF * (h + 1)], listed(t, h), ACT.Copy)
+        def gather_state(dst, t, h):
+            nc.scalar.activation(dst, listed(t, h), ACT.Copy)
 
         for u in units[:3]:
-            nc.scalar.activation(unit(gate, u), u_bank[u][:], ACT.Sigmoid, scale=-1.0)
+            nc.scalar.activation(gate[u], u_bank[u][:], ACT.Sigmoid, scale=-1.0)
         for h in range(2):
-            gather_state(0, h)
-        gate_last = sb.tile([P, 2, HALF], F32, name="gate_last", tag="st0", align_bytes=64)
-        nc.scalar.activation(gate_last[:], u_bank[(1, 1)][:], ACT.Sigmoid, scale=-1.0)
-        for t in (2, 3):
-            for h in range(2):
-                gather_state(t, h)
+            gather_state(base0[:, HALF * h : HALF * (h + 1)], 0, h)
+        gate[(1, 1)] = sb.tile([P, 2, HALF], F32, name="gate_last", tag="st0", align_bytes=64)[:]
+        nc.scalar.activation(gate[(1, 1)], u_bank[(1, 1)][:], ACT.Sigmoid, scale=-1.0)
+        gather_state(base2, 2, 0)
+        gather_state(base3[:], 3, 0)
 
         deal(nc.vector.tensor_copy, 1, 0, 0, 64)
         for tp in range(2):
             deal(nc.vector.tensor_copy, 1, 1, 0, 64, 2 * tp, 2 * tp + 2)
         for tp in range(2):
             quant_w(1, 2 * tp, 2 * tp + 2)
-        keep = sb.tile([P, PACK, S], F32, name="keep", align_bytes=64)
         for h in range(2):
             cols = slice(HALF * h, HALF * (h + 1))
-            nc.vector.tensor_tensor(keep[:, 1, cols], listed(1, h), gate[:, 1, cols], ALU.mult)
+            nc.vector.tensor_tensor(keep[:, 1, cols], listed(1, h), gate01[:, 1, cols], ALU.mult)
         keep0 = sb.tile([P, S], F32, name="keep0", tag="st1", align_bytes=64)
-        nc.gpsimd.tensor_tensor(keep0[:], gate[:, 0, :], base[:, 0, :], ALU.mult)
-        nc.gpsimd.tensor_tensor(keep[:, 2, 0:HALF], gate[:, 2, 0:HALF], base[:, 2, 0:HALF], ALU.mult)
+        nc.gpsimd.tensor_tensor(keep0[:], gate01[:, 0, :], base0[:], ALU.mult)
+        nc.gpsimd.tensor_tensor(keep[:, 2, 0:HALF], gate[(0, 1)][:, 0, :], base2, ALU.mult)
 
         for u in units:
             c_bank = products(1, *u)
-            nc.vector.scalar_tensor_tensor(unit(fresh, u), gate_last[:] if u == (1, 1) else unit(gate, u), 1.0, c_bank[:], ALU.subtract, ALU.mult)
+            nc.vector.scalar_tensor_tensor(unit(fresh, u), gate[u], 1.0, c_bank[:], ALU.subtract, ALU.mult)
 
         y_scales = sb.tile([P, S], U8, name="y_scales", align_bytes=64)
         out_rows = out_0.rearrange("(p t) j -> p t j", t=PACK)
         out_words = out_1[0].rearrange("p n r -> p (n r)").bitcast(I32)
-        y = sb.tile([P, PACK, S], F32, name="y", align_bytes=64)
         pieces = [(0, 0, HALF), (1, 0, QUARTER), (1, QUARTER, HALF)]
         y_bf = [sb.tile([P, PACK * (b - a)], BF16, name="y_bf%d" % i, align_bytes=64) for i, (h, a, b) in enumerate(pieces)]
         y_codes = [sb.tile([P, HALF], U32, name="y_codes%d" % h, align_bytes=64) for h in range(2)]
@@ -166,13 +168,15 @@ def tile_picked_mingru8_none_po_kernel(tc, x_words, x_scales, w1, w2, st, offs, 
             cols = slice(HALF * h + a, HALF * h + b)
             nc.vector.quantize_mx(out=y_codes[h][:, a:b].bitcast(FP8X4), scales=y_scales[:, cols], in_=y_bf[i][:])
 
-        nc.vector.tensor_tensor(keep[:, 3, 0:HALF], gate[:, 3, 0:HALF], base[:, 3, 0:HALF], ALU.mult)
+        nc.vector.tensor_tensor(keep[:, 3, 0:HALF], gate[(0, 1)][:, 1, :], base3[:], ALU.mult)
+        for t in (2, 3):
+            gather_state(keep[:, t, HALF:S], t, 1)
         nc.vector.tensor_tensor(y[:, 0, :], keep0[:], fresh[:, 0, :], ALU.subtract)
         finish(0)
         weave(nc.scalar.copy, 0)
         for h, a, b in pieces[1:]:
             cols = slice(HALF + a, HALF + b)
-            nc.vector.tensor_tensor(keep[:, 2:4, cols], gate_last[:, :, a:b], base[:, 2:4, cols], ALU.mult)
+            nc.vector.tensor_tensor(keep[:, 2:4, cols], gate[(1, 1)][:, :, a:b], keep[:, 2:4, cols], ALU.mult)
         finish(1)
         finish(2)
         weave(nc.scalar.copy, 1)

@@ -19,6 +19,7 @@ P = 128
 PACK = 4
 HALF = S // 2
 QUARTER = S // 4
+W2_FIRST = 320
 SCALAR_DEALT = 24
 
 
@@ -33,7 +34,7 @@ def tile_picked_mingru8_none_po_kernel(tc, x_words, x_scales, w1, w2, st, offs, 
         x_w = sb.tile([P, T], U32, name="x_w", align_bytes=64)
         x_s = sb.tile([P, T], U8, name="x_s", align_bytes=64)
         st_t = [sb.tile([P, S], F32, name="st%d" % t, tag="st%d" % t, align_bytes=64) for t in range(PACK)]
-        w_cuts = [(0, HALF, N), (0, HALF, N)]
+        w_cuts = [(0, HALF, N), (0, W2_FIRST, N)]
         raw = [[sb.tile([P, PACK, b - a], F32, name="raw%d%d" % (w, a), align_bytes=64) for a, b in zip(cuts, cuts[1:])] for w, cuts in enumerate(w_cuts)]
         st_rows = st.rearrange("(p t) j -> p t j", t=PACK)
         w_rows = [w.rearrange("(p j) m -> p j m", j=PACK) for w in (w1, w2)]
@@ -129,9 +130,9 @@ def tile_picked_mingru8_none_po_kernel(tc, x_words, x_scales, w1, w2, st, offs, 
         gather_state(base2, 2, 0)
         gather_state(base3[:], 3, 0)
 
-        deal(nc.vector.tensor_copy, 1, 0, 0, 64)
+        deal(nc.vector.tensor_copy, 1, 0, 0, W2_FIRST // PACK)
         for tp in range(2):
-            deal(nc.vector.tensor_copy, 1, 1, 0, 64, 2 * tp, 2 * tp + 2)
+            deal(nc.vector.tensor_copy, 1, 1, 0, (N - W2_FIRST) // PACK, 2 * tp, 2 * tp + 2)
         for tp in range(2):
             quant_w(1, 2 * tp, 2 * tp + 2)
         for h in range(2):

@@ -56,11 +56,6 @@ def tile_picked_mingru8_none_po_kernel(tc, x_words, x_scales, w1, w2, st, offs, 
         for t in (1, 0, 2, 3):
             nc.sync.dma_start(st_t[t][:], st_rows[:, t, :])
 
-        warm_in = sb.tile([P, 1], F32, name="warm_in")
-        warm_out = sb.tile([P, 1], F32, name="warm_out")
-        nc.vector.memset(warm_in[:], 0.0)
-        nc.scalar.activation(warm_out[:], warm_in[:], ACT.Sigmoid)
-
         w_bf = [sb.tile([P, PACK * N], BF16, name="w_bf%d" % w, align_bytes=64) for w in range(2)]
         w_codes = [sb.tile([P, N], U32, name="w_codes%d" % w, align_bytes=64) for w in range(2)]
         w_scales = [sb.tile([P, N], U8, name="w_scales%d" % w, align_bytes=64) for w in range(2)]
@@ -107,11 +102,10 @@ def tile_picked_mingru8_none_po_kernel(tc, x_words, x_scales, w1, w2, st, offs, 
         u_bank = {u: products(0, *u) for u in units}
         gate01 = sb.tile([P, 2, S], F32, name="gate01", align_bytes=64)
         base0 = sb.tile([P, S], F32, name="base0", align_bytes=64)
-        base3 = sb.tile([P, HALF], F32, name="base3", align_bytes=64)
+        base23 = sb.tile([P, 2, HALF], F32, name="base23", align_bytes=64)
         keep = sb.tile([P, PACK, S], F32, name="keep", align_bytes=64)
         fresh = sb.tile([P, PACK, S], F32, name="fresh", align_bytes=64)
         y = sb.tile([P, PACK, S], F32, name="y", align_bytes=64)
-        base2 = y[:, 0, 0:HALF]
         gate = {(0, 0): gate01[:, :, 0:HALF], (1, 0): gate01[:, :, HALF:S], (0, 1): keep[:, 2:4, HALF:S]}
 
         def unit(tile, u):
@@ -127,8 +121,8 @@ def tile_picked_mingru8_none_po_kernel(tc, x_words, x_scales, w1, w2, st, offs, 
             gather_state(base0[:, HALF * h : HALF * (h + 1)], 0, h)
         gate[(1, 1)] = sb.tile([P, 2, HALF], F32, name="gate_last", tag="st0", align_bytes=64)[:]
         nc.scalar.activation(gate[(1, 1)], u_bank[(1, 1)][:], ACT.Sigmoid, scale=-1.0)
-        gather_state(base2, 2, 0)
-        gather_state(base3[:], 3, 0)
+        for t in (2, 3):
+            gather_state(base23[:, t - 2, :], t, 0)
 
         deal(nc.vector.tensor_copy, 1, 0, 0, W2_FIRST // PACK)
         for tp in range(2):
@@ -140,7 +134,6 @@ def tile_picked_mingru8_none_po_kernel(tc, x_words, x_scales, w1, w2, st, offs, 
             nc.vector.tensor_tensor(keep[:, 1, cols], listed(1, h), gate01[:, 1, cols], ALU.mult)
         keep0 = sb.tile([P, S], F32, name="keep0", tag="st1", align_bytes=64)
         nc.gpsimd.tensor_tensor(keep0[:], gate01[:, 0, :], base0[:], ALU.mult)
-        nc.gpsimd.tensor_tensor(keep[:, 2, 0:HALF], gate[(0, 1)][:, 0, :], base2, ALU.mult)
 
         for u in units:
             c_bank = products(1, *u)
@@ -169,7 +162,8 @@ def tile_picked_mingru8_none_po_kernel(tc, x_words, x_scales, w1, w2, st, offs, 
             cols = slice(HALF * h + a, HALF * h + b)
             nc.vector.quantize_mx(out=y_codes[h][:, a:b].bitcast(FP8X4), scales=y_scales[:, cols], in_=y_bf[i][:])
 
-        nc.vector.tensor_tensor(keep[:, 3, 0:HALF], gate[(0, 1)][:, 1, :], base3[:], ALU.mult)
+        for t in (2, 3):
+            nc.vector.tensor_tensor(keep[:, t, 0:HALF], gate[(0, 1)][:, t - 2, :], base23[:, t - 2, :], ALU.mult)
         for t in (2, 3):
             gather_state(keep[:, t, HALF:S], t, 1)
         nc.vector.tensor_tensor(y[:, 0, :], keep0[:], fresh[:, 0, :], ALU.subtract)

@@ -53,7 +53,7 @@ def tile_picked_mingru8_none_po_kernel(tc, x_words, x_scales, w1, w2, st, offs, 
         for h in range(2):
             load_w(1, h)
         nc.sync.dma_start(par_t[:], par)
-        for t in (1, 0, 2, 3):
+        for t in range(PACK):
             nc.sync.dma_start(st_t[t][:], st_rows[:, t, :])
 
         w_bf = [sb.tile([P, PACK * N], BF16, name="w_bf%d" % w, align_bytes=64) for w in range(2)]
@@ -70,18 +70,19 @@ def tile_picked_mingru8_none_po_kernel(tc, x_words, x_scales, w1, w2, st, offs, 
             nc.vector.quantize_mx(out=w_codes[w][:, cols].bitcast(FP8X4), scales=w_scales[w][:, cols], in_=w_bf[w][:, PACK * P * t0 : PACK * P * t1])
 
         xg_w = [sb.tile([P, HALF], U32, name="xg_w%d" % h, align_bytes=64) for h in range(2)]
+        token_cuts = [(0, 0, QUARTER), (0, QUARTER, HALF), (1, 0, HALF)]
         xg_s = sb.tile([P, S], U8, name="xg_s", align_bytes=64)
 
-        def products(w, h, tp):
-            bank = ps.tile([P, 2, HALF], F32, name="bank%d%d%d" % (w, h, tp))
-            for i in range(2):
-                cols = slice(P * (2 * tp + i), P * (2 * tp + i + 1))
+        def products(w, h, t0, t1, a=0, b=HALF):
+            bank = ps.tile([P, t1 - t0, b - a], F32, name="bank%d%d%d%d" % (w, h, t0, a))
+            for t in range(t0, t1):
+                cols = slice(P * t, P * (t + 1))
                 nc.tensor.matmul_mx(
-                    out=bank[:, i, :],
+                    out=bank[:, t - t0, :],
                     lhsT=w_codes[w][:, cols].bitcast(FP8X4),
                     lhsT_scale=w_scales[w][:, cols],
-                    rhs=xg_w[h][:].bitcast(FP8X4),
-                    rhs_scale=xg_s[:, HALF * h : HALF * (h + 1)],
+                    rhs=xg_w[h][:, a:b].bitcast(FP8X4),
+                    rhs_scale=xg_s[:, HALF * h + a : HALF * h + b],
                     start=True,
                     stop=True,
                 )
@@ -95,49 +96,55 @@ def tile_picked_mingru8_none_po_kernel(tc, x_words, x_scales, w1, w2, st, offs, 
         deal(nc.scalar.copy, 0, 1, 0, SCALAR_DEALT)
         deal(nc.vector.tensor_copy, 0, 1, SCALAR_DEALT, 64)
         quant_w(0)
-        for h in range(2):
-            nc.vector.tensor_copy(xg_w[h][:], x_w[:].indirect(offs_t[:, 16 * h : 16 * (h + 1)]))
+        for h, a, b in token_cuts:
+            nc.vector.tensor_copy(xg_w[h][:, a:b], x_w[:].indirect(offs_t[:, (HALF * h + a) // 16 : (HALF * h + b) // 16]))
 
-        units = [(h, tp) for h in range(2) for tp in range(2)]
-        u_bank = {u: products(0, *u) for u in units}
-        gate01 = sb.tile([P, 2, S], F32, name="gate01", align_bytes=64)
-        base0 = sb.tile([P, S], F32, name="base0", align_bytes=64)
-        base23 = sb.tile([P, 2, HALF], F32, name="base23", align_bytes=64)
-        keep = sb.tile([P, PACK, S], F32, name="keep", align_bytes=64)
-        fresh = sb.tile([P, PACK, S], F32, name="fresh", align_bytes=64)
-        y = sb.tile([P, PACK, S], F32, name="y", align_bytes=64)
-        gate = {(0, 0): gate01[:, :, 0:HALF], (1, 0): gate01[:, :, HALF:S], (0, 1): keep[:, 2:4, HALF:S]}
+        units = [(h, pair) for h in range(2) for pair in range(2)]
+        u_first = [products(0, 0, 0, PACK, a, b) for h, a, b in token_cuts[:2]]
+        u_bank = [products(0, 1, 2 * pair, 2 * pair + 2) for pair in range(2)]
+        gate0 = sb.tile([P, PACK, HALF], F32, name="gate0", align_bytes=64)
+        gate1 = [sb.tile([P, 2, HALF], F32, name="gate10", align_bytes=64)[:]]
+        fresh = [sb.tile([P, PACK, HALF], F32, name="fresh%d" % h, align_bytes=64) for h in range(2)]
+        picked = sb.tile([P, PACK, HALF], F32, name="picked", align_bytes=64)
+        keep = sb.tile([P, PACK, HALF], F32, name="keep", align_bytes=64)
+        keep_first = sb.tile([P, HALF], F32, name="keep_first", align_bytes=64)
 
-        def unit(tile, u):
-            h, tp = u
-            return tile[:, 2 * tp : 2 * tp + 2, HALF * h : HALF * (h + 1)]
+        def gate_of(h, pair):
+            return gate1[pair] if h else gate0[:, 2 * pair : 2 * pair + 2, :]
+
+        def make_gate(dst, bank):
+            nc.scalar.activation(dst, bank[:], ACT.Sigmoid, scale=-1.0)
+
+        def make_fresh(h, pair):
+            nc.vector.scalar_tensor_tensor(fresh[h][:, 2 * pair : 2 * pair + 2, :], gate_of(h, pair), 1.0, c_bank[(h, pair)][:], ALU.subtract, ALU.mult)
 
         def gather_state(dst, t, h):
             nc.scalar.activation(dst, listed(t, h), ACT.Copy)
 
-        for u in units[:3]:
-            nc.scalar.activation(gate[u], u_bank[u][:], ACT.Sigmoid, scale=-1.0)
-        for h in range(2):
-            gather_state(base0[:, HALF * h : HALF * (h + 1)], 0, h)
-        gate[(1, 1)] = sb.tile([P, 2, HALF], F32, name="gate_last", tag="st0", align_bytes=64)[:]
-        nc.scalar.activation(gate[(1, 1)], u_bank[(1, 1)][:], ACT.Sigmoid, scale=-1.0)
-        for t in (2, 3):
-            gather_state(base23[:, t - 2, :], t, 0)
+        for bank, (h, a, b) in zip(u_first, token_cuts):
+            make_gate(gate0[:, :, a:b], bank)
+        make_gate(gate1[0], u_bank[0])
+        for t in range(1, PACK):
+            gather_state(picked[:, t - 1, :], t, 0)
+        gather_state(picked[:, 3, :], 3, 1)
+        late = sb.tile([P, PACK + 3, HALF], F32, name="late", tag="st3", align_bytes=64)
+        y_last = sb.tile([P, PACK, HALF], F32, name="y_last", align_bytes=64)
+        y = [late[:, 3:, :], y_last[:]]
+        gate1.append(late[:, 1:3, :])
+        make_gate(gate1[1], u_bank[1])
+        gather_state(late[:, 0, :], 1, 1)
 
         deal(nc.vector.tensor_copy, 1, 0, 0, W2_FIRST // PACK)
-        for tp in range(2):
-            deal(nc.vector.tensor_copy, 1, 1, 0, (N - W2_FIRST) // PACK, 2 * tp, 2 * tp + 2)
-        for tp in range(2):
-            quant_w(1, 2 * tp, 2 * tp + 2)
-        for h in range(2):
-            cols = slice(HALF * h, HALF * (h + 1))
-            nc.vector.tensor_tensor(keep[:, 1, cols], listed(1, h), gate01[:, 1, cols], ALU.mult)
-        keep0 = sb.tile([P, S], F32, name="keep0", tag="st1", align_bytes=64)
-        nc.gpsimd.tensor_tensor(keep0[:], gate01[:, 0, :], base0[:], ALU.mult)
-
-        for u in units:
-            c_bank = products(1, *u)
-            nc.vector.scalar_tensor_tensor(unit(fresh, u), gate[u], 1.0, c_bank[:], ALU.subtract, ALU.mult)
+        for pair in range(2):
+            deal(nc.vector.tensor_copy, 1, 1, 0, (N - W2_FIRST) // PACK, 2 * pair, 2 * pair + 2)
+        for pair in range(2):
+            quant_w(1, 2 * pair, 2 * pair + 2)
+        c_bank = {(h, pair): products(1, h, 2 * pair, 2 * pair + 2) for h, pair in units}
+        nc.vector.tensor_tensor(keep_first[:], listed(0, 0), gate0[:, 0, :], ALU.mult)
+        nc.vector.tensor_tensor(keep[:, 0, :], listed(0, 1), gate1[0][:, 0, :], ALU.mult)
+        nc.gpsimd.tensor_tensor(keep[:, 1:3, :], gate0[:, 1:3, :], picked[:, 0:2, :], ALU.mult)
+        for u in units[:3]:
+            make_fresh(*u)
 
         y_scales = sb.tile([P, S], U8, name="y_scales", align_bytes=64)
         out_rows = out_0.rearrange("(p t) j -> p t j", t=PACK)
@@ -146,34 +153,32 @@ def tile_picked_mingru8_none_po_kernel(tc, x_words, x_scales, w1, w2, st, offs, 
         y_bf = [sb.tile([P, PACK * (b - a)], BF16, name="y_bf%d" % i, align_bytes=64) for i, (h, a, b) in enumerate(pieces)]
         y_codes = [sb.tile([P, HALF], U32, name="y_codes%d" % h, align_bytes=64) for h in range(2)]
 
-        def finish(i):
+        def store_y(i):
             h, a, b = pieces[i]
-            cols = slice(HALF * h + a, HALF * h + b)
-            nc.vector.tensor_tensor(y[:, 1:PACK, cols], keep[:, 1:PACK, cols], fresh[:, 1:PACK, cols], ALU.subtract)
-            nc.sync.dma_start(out_rows[:, :, cols], y[:, :, cols])
+            nc.sync.dma_start(out_rows[:, :, HALF * h + a : HALF * h + b], y[h][:, :, a:b])
 
         def weave(copy, i):
             h, a, b = pieces[i]
-            cols = slice(HALF * h + a, HALF * h + b)
-            copy(y_bf[i][:].rearrange("p (c i t) -> p c t i", i=4, t=PACK), y[:, :, cols].rearrange("p t (c i) -> p c t i", i=4))
+            copy(y_bf[i][:].rearrange("p (c i t) -> p c t i", i=4, t=PACK), y[h][:, :, a:b].rearrange("p t (c i) -> p c t i", i=4))
 
         def quant_y(i):
             h, a, b = pieces[i]
-            cols = slice(HALF * h + a, HALF * h + b)
-            nc.vector.quantize_mx(out=y_codes[h][:, a:b].bitcast(FP8X4), scales=y_scales[:, cols], in_=y_bf[i][:])
+            nc.vector.quantize_mx(out=y_codes[h][:, a:b].bitcast(FP8X4), scales=y_scales[:, HALF * h + a : HALF * h + b], in_=y_bf[i][:])
 
-        for t in (2, 3):
-            nc.vector.tensor_tensor(keep[:, t, 0:HALF], gate[(0, 1)][:, t - 2, :], base23[:, t - 2, :], ALU.mult)
-        for t in (2, 3):
-            gather_state(keep[:, t, HALF:S], t, 1)
-        nc.vector.tensor_tensor(y[:, 0, :], keep0[:], fresh[:, 0, :], ALU.subtract)
-        finish(0)
+        nc.vector.tensor_tensor(keep[:, 3, :], gate0[:, 3, :], picked[:, 2, :], ALU.mult)
+        gather_state(picked[:, 2, :], 2, 1)
+        nc.vector.tensor_tensor(y[0][:, 0, :], keep_first[:], fresh[0][:, 0, :], ALU.subtract)
+        nc.vector.tensor_tensor(y[0][:, 1:PACK, :], keep[:, 1:PACK, :], fresh[0][:, 1:PACK, :], ALU.subtract)
+        store_y(0)
         weave(nc.scalar.copy, 0)
+        make_fresh(1, 1)
+        nc.vector.tensor_tensor(keep[:, 1, :], gate1[0][:, 1, :], late[:, 0, :], ALU.mult)
         for h, a, b in pieces[1:]:
-            cols = slice(HALF + a, HALF + b)
-            nc.vector.tensor_tensor(keep[:, 2:4, cols], gate[(1, 1)][:, :, a:b], keep[:, 2:4, cols], ALU.mult)
-        finish(1)
-        finish(2)
+            nc.vector.tensor_tensor(keep[:, 2:4, a:b], gate1[1][:, :, a:b], picked[:, 2:4, a:b], ALU.mult)
+        for i in (1, 2):
+            h, a, b = pieces[i]
+            nc.vector.tensor_tensor(y[1][:, :, a:b], keep[:, :, a:b], fresh[1][:, :, a:b], ALU.subtract)
+            store_y(i)
         weave(nc.scalar.copy, 1)
         quant_y(0)
         nc.scalar.dma_start(out_words[:, 0:HALF], y_codes[0][:].bitcast(I32))

@@ -21,6 +21,7 @@ HALF = S // 2
 QUARTER = S // 4
 W2_FIRST = 320
 SCALAR_DEALT = 24
+SCALAR_RUNS = 16
 
 
 def tile_picked_mingru8_none_po_kernel(tc, x_words, x_scales, w1, w2, st, offs, par, out_0, out_1, out_2):
@@ -142,7 +143,8 @@ def tile_picked_mingru8_none_po_kernel(tc, x_words, x_scales, w1, w2, st, offs, 
         c_bank = {(h, pair): products(1, h, 2 * pair, 2 * pair + 2) for h, pair in units}
         nc.vector.tensor_tensor(keep_first[:], listed(0, 0), gate0[:, 0, :], ALU.mult)
         nc.vector.tensor_tensor(keep[:, 0, :], listed(0, 1), gate1[0][:, 0, :], ALU.mult)
-        nc.gpsimd.tensor_tensor(keep[:, 1:3, :], gate0[:, 1:3, :], picked[:, 0:2, :], ALU.mult)
+        for t in (1, 2):
+            nc.gpsimd.tensor_tensor(keep[:, t, :], gate0[:, t, :], picked[:, t - 1, :], ALU.mult)
         for u in units[:3]:
             make_fresh(*u)
 
@@ -157,9 +159,10 @@ def tile_picked_mingru8_none_po_kernel(tc, x_words, x_scales, w1, w2, st, offs, 
             h, a, b = pieces[i]
             nc.sync.dma_start(out_rows[:, :, HALF * h + a : HALF * h + b], y[h][:, :, a:b])
 
-        def weave(copy, i):
+        def weave(copy, i, first=0, last=None):
             h, a, b = pieces[i]
-            copy(y_bf[i][:].rearrange("p (c i t) -> p c t i", i=4, t=PACK), y[h][:, :, a:b].rearrange("p t (c i) -> p c t i", i=4))
+            runs = slice(first, last)
+            copy(y_bf[i][:].rearrange("p (c i t) -> p c t i", i=4, t=PACK)[:, runs], y[h][:, :, a:b].rearrange("p t (c i) -> p c t i", i=4)[:, runs])
 
         def quant_y(i):
             h, a, b = pieces[i]
@@ -180,9 +183,10 @@ def tile_picked_mingru8_none_po_kernel(tc, x_words, x_scales, w1, w2, st, offs, 
             nc.vector.tensor_tensor(y[1][:, :, a:b], keep[:, :, a:b], fresh[1][:, :, a:b], ALU.subtract)
             store_y(i)
         weave(nc.scalar.copy, 1)
+        weave(nc.scalar.copy, 2, 0, SCALAR_RUNS)
         quant_y(0)
         nc.scalar.dma_start(out_words[:, 0:HALF], y_codes[0][:].bitcast(I32))
-        weave(nc.vector.tensor_copy, 2)
+        weave(nc.vector.tensor_copy, 2, SCALAR_RUNS)
         quant_y(1)
         quant_y(2)
         nc.scalar.dma_start(out_words[:, HALF:S], y_codes[1][:].bitcast(I32))

@@ -21,7 +21,6 @@ HALF = S // 2
 QUARTER = S // 4
 W2_FIRST = 320
 SCALAR_DEALT = 24
-SCALAR_RUNS = 16
 
 
 def tile_picked_mingru8_none_po_kernel(tc, x_words, x_scales, w1, w2, st, offs, par, out_0, out_1, out_2):
@@ -103,37 +102,30 @@ def tile_picked_mingru8_none_po_kernel(tc, x_words, x_scales, w1, w2, st, offs, 
         units = [(h, pair) for h in range(2) for pair in range(2)]
         u_first = [products(0, 0, 0, PACK, a, b) for h, a, b in token_cuts[:2]]
         u_bank = [products(0, 1, 2 * pair, 2 * pair + 2) for pair in range(2)]
-        gate0 = sb.tile([P, PACK, HALF], F32, name="gate0", align_bytes=64)
-        gate1 = [sb.tile([P, 2, HALF], F32, name="gate10", align_bytes=64)[:]]
+        gate = [sb.tile([P, PACK, HALF], F32, name="gate%d" % h, align_bytes=64) for h in range(2)]
         fresh = [sb.tile([P, PACK, HALF], F32, name="fresh%d" % h, align_bytes=64) for h in range(2)]
+        keep = [sb.tile([P, PACK, HALF], F32, name="keep%d" % h, align_bytes=64) for h in range(2)]
         picked = sb.tile([P, PACK, HALF], F32, name="picked", align_bytes=64)
-        keep = sb.tile([P, PACK, HALF], F32, name="keep", align_bytes=64)
-        keep_first = sb.tile([P, HALF], F32, name="keep_first", align_bytes=64)
-
-        def gate_of(h, pair):
-            return gate1[pair] if h else gate0[:, 2 * pair : 2 * pair + 2, :]
 
         def make_gate(dst, bank):
             nc.scalar.activation(dst, bank[:], ACT.Sigmoid, scale=-1.0)
 
         def make_fresh(h, pair):
-            nc.vector.scalar_tensor_tensor(fresh[h][:, 2 * pair : 2 * pair + 2, :], gate_of(h, pair), 1.0, c_bank[(h, pair)][:], ALU.subtract, ALU.mult)
+            planes = slice(2 * pair, 2 * pair + 2)
+            nc.vector.scalar_tensor_tensor(fresh[h][:, planes, :], gate[h][:, planes, :], 1.0, c_bank[(h, pair)][:], ALU.subtract, ALU.mult)
 
         def gather_state(dst, t, h):
             nc.scalar.activation(dst, listed(t, h), ACT.Copy)
 
         for bank, (h, a, b) in zip(u_first, token_cuts):
-            make_gate(gate0[:, :, a:b], bank)
-        make_gate(gate1[0], u_bank[0])
+            make_gate(gate[0][:, :, a:b], bank)
+        for pair in range(2):
+            make_gate(gate[1][:, 2 * pair : 2 * pair + 2, :], u_bank[pair])
         for t in range(1, PACK):
             gather_state(picked[:, t - 1, :], t, 0)
         gather_state(picked[:, 3, :], 3, 1)
-        late = sb.tile([P, PACK + 3, HALF], F32, name="late", tag="st3", align_bytes=64)
-        y_last = sb.tile([P, PACK, HALF], F32, name="y_last", align_bytes=64)
-        y = [late[:, 3:, :], y_last[:]]
-        gate1.append(late[:, 1:3, :])
-        make_gate(gate1[1], u_bank[1])
-        gather_state(late[:, 0, :], 1, 1)
+        y = [sb.tile([P, PACK, HALF], F32, name="y%d" % h, tag=tag, align_bytes=64)[:] for h, tag in enumerate(("st3", "y1"))]
+        second = [picked[:, 1, :], gate[0][:, 2, :], picked[:, 2, :], picked[:, 3, :]]
 
         deal(nc.vector.tensor_copy, 1, 0, 0, W2_FIRST // PACK)
         for pair in range(2):
@@ -141,12 +133,13 @@ def tile_picked_mingru8_none_po_kernel(tc, x_words, x_scales, w1, w2, st, offs, 
         for pair in range(2):
             quant_w(1, 2 * pair, 2 * pair + 2)
         c_bank = {(h, pair): products(1, h, 2 * pair, 2 * pair + 2) for h, pair in units}
-        nc.vector.tensor_tensor(keep_first[:], listed(0, 0), gate0[:, 0, :], ALU.mult)
-        nc.vector.tensor_tensor(keep[:, 0, :], listed(0, 1), gate1[0][:, 0, :], ALU.mult)
+        nc.vector.tensor_tensor(keep[0][:, 0, :], listed(0, 0), gate[0][:, 0, :], ALU.mult)
         for t in (1, 2):
-            nc.gpsimd.tensor_tensor(keep[:, t, :], gate0[:, t, :], picked[:, t - 1, :], ALU.mult)
-        for u in units[:3]:
+            nc.gpsimd.tensor_tensor(keep[0][:, t, :], gate[0][:, t, :], picked[:, t - 1, :], ALU.mult)
+        for u in units:
             make_fresh(*u)
+        for t in range(2):
+            gather_state(second[t], t, 1)
 
         y_scales = sb.tile([P, S], U8, name="y_scales", align_bytes=64)
         out_rows = out_0.rearrange("(p t) j -> p t j", t=PACK)
@@ -155,38 +148,34 @@ def tile_picked_mingru8_none_po_kernel(tc, x_words, x_scales, w1, w2, st, offs, 
         y_bf = [sb.tile([P, PACK * (b - a)], BF16, name="y_bf%d" % i, align_bytes=64) for i, (h, a, b) in enumerate(pieces)]
         y_codes = [sb.tile([P, HALF], U32, name="y_codes%d" % h, align_bytes=64) for h in range(2)]
 
-        def store_y(i):
+        def weave(copy, i):
             h, a, b = pieces[i]
-            nc.sync.dma_start(out_rows[:, :, HALF * h + a : HALF * h + b], y[h][:, :, a:b])
-
-        def weave(copy, i, first=0, last=None):
-            h, a, b = pieces[i]
-            runs = slice(first, last)
-            copy(y_bf[i][:].rearrange("p (c i t) -> p c t i", i=4, t=PACK)[:, runs], y[h][:, :, a:b].rearrange("p t (c i) -> p c t i", i=4)[:, runs])
+            copy(y_bf[i][:].rearrange("p (c i t) -> p c t i", i=4, t=PACK), y[h][:, :, a:b].rearrange("p t (c i) -> p c t i", i=4))
 
         def quant_y(i):
             h, a, b = pieces[i]
             nc.vector.quantize_mx(out=y_codes[h][:, a:b].bitcast(FP8X4), scales=y_scales[:, HALF * h + a : HALF * h + b], in_=y_bf[i][:])
 
-        nc.vector.tensor_tensor(keep[:, 3, :], gate0[:, 3, :], picked[:, 2, :], ALU.mult)
+        nc.vector.tensor_tensor(keep[0][:, 3, :], gate[0][:, 3, :], picked[:, 2, :], ALU.mult)
         gather_state(picked[:, 2, :], 2, 1)
-        nc.vector.tensor_tensor(y[0][:, 0, :], keep_first[:], fresh[0][:, 0, :], ALU.subtract)
-        nc.vector.tensor_tensor(y[0][:, 1:PACK, :], keep[:, 1:PACK, :], fresh[0][:, 1:PACK, :], ALU.subtract)
-        store_y(0)
+        for planes in (slice(0, 1), slice(1, PACK)):
+            nc.vector.tensor_tensor(y[0][:, planes, :], keep[0][:, planes, :], fresh[0][:, planes, :], ALU.subtract)
+        nc.sync.dma_start(out_rows[:, :, 0:HALF], y[0])
         weave(nc.scalar.copy, 0)
-        make_fresh(1, 1)
-        nc.vector.tensor_tensor(keep[:, 1, :], gate1[0][:, 1, :], late[:, 0, :], ALU.mult)
+        outer = slice(0, PACK, PACK - 1)
+        nc.vector.tensor_tensor(keep[1][:, outer, :], gate[1][:, outer, :], picked[:, 1:PACK:2, :], ALU.mult)
+        nc.vector.tensor_tensor(keep[1][:, 1, :], gate[1][:, 1, :], second[1], ALU.mult)
+        nc.vector.tensor_tensor(y[1][:, 3, :], keep[1][:, 3, :], fresh[1][:, 3, :], ALU.subtract)
+        nc.vector.tensor_tensor(keep[1][:, 2, :], gate[1][:, 2, :], second[2], ALU.mult)
+        nc.vector.tensor_tensor(y[1][:, 0, :], keep[1][:, 0, :], fresh[1][:, 0, :], ALU.subtract)
+        nc.sync.dma_start(out_rows[:, outer, HALF:S], y[1][:, outer, :])
         for h, a, b in pieces[1:]:
-            nc.vector.tensor_tensor(keep[:, 2:4, a:b], gate1[1][:, :, a:b], picked[:, 2:4, a:b], ALU.mult)
-        for i in (1, 2):
-            h, a, b = pieces[i]
-            nc.vector.tensor_tensor(y[1][:, :, a:b], keep[:, :, a:b], fresh[1][:, :, a:b], ALU.subtract)
-            store_y(i)
+            nc.vector.tensor_tensor(y[1][:, 1:3, a:b], keep[1][:, 1:3, a:b], fresh[1][:, 1:3, a:b], ALU.subtract)
+        nc.sync.dma_start(out_rows[:, 1:3, HALF:S], y[1][:, 1:3, :])
         weave(nc.scalar.copy, 1)
-        weave(nc.scalar.copy, 2, 0, SCALAR_RUNS)
         quant_y(0)
         nc.scalar.dma_start(out_words[:, 0:HALF], y_codes[0][:].bitcast(I32))
-        weave(nc.vector.tensor_copy, 2, SCALAR_RUNS)
+        weave(nc.vector.tensor_copy, 2)
         quant_y(1)
         quant_y(2)
         nc.scalar.dma_start(out_words[:, HALF:S], y_codes[1][:].bitcast(I32))

@@ -21,6 +21,7 @@ HALF = S // 2
 QUARTER = S // 4
 W2_FIRST = 320
 SCALAR_DEALT = 24
+SCALAR_RUNS = 16
 
 
 def tile_picked_mingru8_none_po_kernel(tc, x_words, x_scales, w1, w2, st, offs, par, out_0, out_1, out_2):
@@ -148,9 +149,10 @@ def tile_picked_mingru8_none_po_kernel(tc, x_words, x_scales, w1, w2, st, offs, 
         y_bf = [sb.tile([P, PACK * (b - a)], BF16, name="y_bf%d" % i, align_bytes=64) for i, (h, a, b) in enumerate(pieces)]
         y_codes = [sb.tile([P, HALF], U32, name="y_codes%d" % h, align_bytes=64) for h in range(2)]
 
-        def weave(copy, i):
+        def weave(copy, i, first=0, last=None):
             h, a, b = pieces[i]
-            copy(y_bf[i][:].rearrange("p (c i t) -> p c t i", i=4, t=PACK), y[h][:, :, a:b].rearrange("p t (c i) -> p c t i", i=4))
+            runs = slice(first, last)
+            copy(y_bf[i][:].rearrange("p (c i t) -> p c t i", i=4, t=PACK)[:, runs], y[h][:, :, a:b].rearrange("p t (c i) -> p c t i", i=4)[:, runs])
 
         def quant_y(i):
             h, a, b = pieces[i]
@@ -173,9 +175,10 @@ def tile_picked_mingru8_none_po_kernel(tc, x_words, x_scales, w1, w2, st, offs, 
             nc.vector.tensor_tensor(y[1][:, 1:3, a:b], keep[1][:, 1:3, a:b], fresh[1][:, 1:3, a:b], ALU.subtract)
         nc.sync.dma_start(out_rows[:, 1:3, HALF:S], y[1][:, 1:3, :])
         weave(nc.scalar.copy, 1)
+        weave(nc.scalar.copy, 2, 0, SCALAR_RUNS)
         quant_y(0)
         nc.scalar.dma_start(out_words[:, 0:HALF], y_codes[0][:].bitcast(I32))
-        weave(nc.vector.tensor_copy, 2)
+        weave(nc.vector.tensor_copy, 2, SCALAR_RUNS)
         quant_y(1)
         quant_y(2)
         nc.scalar.dma_start(out_words[:, HALF:S], y_codes[1][:].bitcast(I32))

@@ -20,7 +20,6 @@ PACK = 4
 HALF = S // 2
 QUARTER = S // 4
 W2_FIRST = 320
-SCALAR_DEALT = 24
 SCALAR_RUNS = 16
 
 
@@ -61,9 +60,9 @@ def tile_picked_mingru8_none_po_kernel(tc, x_words, x_scales, w1, w2, st, offs, 
         w_codes = [sb.tile([P, N], U32, name="w_codes%d" % w, align_bytes=64) for w in range(2)]
         w_scales = [sb.tile([P, N], U8, name="w_scales%d" % w, align_bytes=64) for w in range(2)]
 
-        def deal(copy, w, h, a, b, t0=0, t1=PACK):
-            dst = w_bf[w][:].rearrange("p (t m j) -> p m j t", t=PACK, j=PACK)[:, w_cuts[w][h] // PACK + a : w_cuts[w][h] // PACK + b, :, t0:t1]
-            src = raw[w][h][:].rearrange("p j (m t) -> p m j t", t=PACK)[:, a:b, :, t0:t1]
+        def deal(copy, w, h, t0=0, t1=PACK):
+            dst = w_bf[w][:].rearrange("p (t m j) -> p m j t", t=PACK, j=PACK)[:, w_cuts[w][h] // PACK : w_cuts[w][h + 1] // PACK, :, t0:t1]
+            src = raw[w][h][:].rearrange("p j (m t) -> p m j t", t=PACK)[:, :, :, t0:t1]
             copy(dst, src)
 
         def quant_w(w, t0=0, t1=PACK):
@@ -92,10 +91,9 @@ def tile_picked_mingru8_none_po_kernel(tc, x_words, x_scales, w1, w2, st, offs, 
         def listed(t, h):
             return st_t[t][:].indirect(par_t[:, 16 * h : 16 * (h + 1)])
 
-        deal(nc.vector.tensor_copy, 0, 0, 0, 64)
+        deal(nc.scalar.copy, 0, 0)
         nc.vector.tensor_copy(xg_s[:], x_s[:].indirect(offs_t[:]))
-        deal(nc.scalar.copy, 0, 1, 0, SCALAR_DEALT)
-        deal(nc.vector.tensor_copy, 0, 1, SCALAR_DEALT, 64)
+        deal(nc.vector.tensor_copy, 0, 1)
         quant_w(0)
         for h, a, b in token_cuts:
             nc.vector.tensor_copy(xg_w[h][:, a:b], x_w[:].indirect(offs_t[:, (HALF * h + a) // 16 : (HALF * h + b) // 16]))
@@ -128,9 +126,9 @@ def tile_picked_mingru8_none_po_kernel(tc, x_words, x_scales, w1, w2, st, offs, 
         y = [sb.tile([P, PACK, HALF], F32, name="y%d" % h, tag=tag, align_bytes=64)[:] for h, tag in enumerate(("st3", "y1"))]
         second = [picked[:, 1, :], gate[0][:, 2, :], picked[:, 2, :], picked[:, 3, :]]
 
-        deal(nc.vector.tensor_copy, 1, 0, 0, W2_FIRST // PACK)
+        deal(nc.vector.tensor_copy, 1, 0)
         for pair in range(2):
-            deal(nc.vector.tensor_copy, 1, 1, 0, (N - W2_FIRST) // PACK, 2 * pair, 2 * pair + 2)
+            deal(nc.vector.tensor_copy, 1, 1, 2 * pair, 2 * pair + 2)
         for pair in range(2):
             quant_w(1, 2 * pair, 2 * pair + 2)
         c_bank = {(h, pair): products(1, h, 2 * pair, 2 * pair + 2) for h, pair in units}

@@ -20,7 +20,6 @@ PACK = 4
 HALF = S // 2
 QUARTER = S // 4
 W2_FIRST = 320
-SCALAR_RUNS = 16
 
 
 def tile_picked_mingru8_none_po_kernel(tc, x_words, x_scales, w1, w2, st, offs, par, out_0, out_1, out_2):
@@ -34,13 +33,14 @@ def tile_picked_mingru8_none_po_kernel(tc, x_words, x_scales, w1, w2, st, offs, 
         x_w = sb.tile([P, T], U32, name="x_w", align_bytes=64)
         x_s = sb.tile([P, T], U8, name="x_s", align_bytes=64)
         st_t = [sb.tile([P, S], F32, name="st%d" % t, tag="st%d" % t, align_bytes=64) for t in range(PACK)]
-        w_cuts = [(0, HALF, N), (0, W2_FIRST, N)]
-        raw = [[sb.tile([P, PACK, b - a], F32, name="raw%d%d" % (w, a), align_bytes=64) for a, b in zip(cuts, cuts[1:])] for w, cuts in enumerate(w_cuts)]
+        w_pieces = [[(0, 2, 0, N), (2, PACK, 0, N)], [(0, PACK, 0, W2_FIRST), (0, PACK, W2_FIRST, N)]]
+        raw = [[sb.tile([P, j1 - j0, b - a], F32, name="raw%d%d" % (w, h), align_bytes=64) for h, (j0, j1, a, b) in enumerate(pieces)] for w, pieces in enumerate(w_pieces)]
         st_rows = st.rearrange("(p t) j -> p t j", t=PACK)
         w_rows = [w.rearrange("(p j) m -> p j m", j=PACK) for w in (w1, w2)]
 
         def load_w(w, h):
-            nc.sync.dma_start(raw[w][h][:], w_rows[w][:, :, w_cuts[w][h] : w_cuts[w][h + 1]])
+            j0, j1, a, b = w_pieces[w][h]
+            nc.sync.dma_start(raw[w][h][:], w_rows[w][:, j0:j1, a:b])
 
         nc.vector.memset(x_s[:].bitcast(I32), 0)
 
@@ -61,7 +61,8 @@ def tile_picked_mingru8_none_po_kernel(tc, x_words, x_scales, w1, w2, st, offs, 
         w_scales = [sb.tile([P, N], U8, name="w_scales%d" % w, align_bytes=64) for w in range(2)]
 
         def deal(copy, w, h, t0=0, t1=PACK):
-            dst = w_bf[w][:].rearrange("p (t m j) -> p m j t", t=PACK, j=PACK)[:, w_cuts[w][h] // PACK : w_cuts[w][h + 1] // PACK, :, t0:t1]
+            j0, j1, a, b = w_pieces[w][h]
+            dst = w_bf[w][:].rearrange("p (t m j) -> p m j t", t=PACK, j=PACK)[:, a // PACK : b // PACK, j0:j1, t0:t1]
             src = raw[w][h][:].rearrange("p j (m t) -> p m j t", t=PACK)[:, :, :, t0:t1]
             copy(dst, src)
 
@@ -91,10 +92,13 @@ def tile_picked_mingru8_none_po_kernel(tc, x_words, x_scales, w1, w2, st, offs, 
         def listed(t, h):
             return st_t[t][:].indirect(par_t[:, 16 * h : 16 * (h + 1)])
 
-        deal(nc.scalar.copy, 0, 0)
+        for h in range(2):
+            deal(nc.scalar.copy, 0, h, 0, 2)
+        deal(nc.vector.tensor_copy, 0, 0, 2, PACK)
         nc.vector.tensor_copy(xg_s[:], x_s[:].indirect(offs_t[:]))
-        deal(nc.vector.tensor_copy, 0, 1)
-        quant_w(0)
+        deal(nc.vector.tensor_copy, 0, 1, 2, PACK)
+        for pair in range(2):
+            quant_w(0, 2 * pair, 2 * pair + 2)
         for h, a, b in token_cuts:
             nc.vector.tensor_copy(xg_w[h][:, a:b], x_w[:].indirect(offs_t[:, (HALF * h + a) // 16 : (HALF * h + b) // 16]))
 
@@ -147,10 +151,9 @@ def tile_picked_mingru8_none_po_kernel(tc, x_words, x_scales, w1, w2, st, offs, 
         y_bf = [sb.tile([P, PACK * (b - a)], BF16, name="y_bf%d" % i, align_bytes=64) for i, (h, a, b) in enumerate(pieces)]
         y_codes = [sb.tile([P, HALF], U32, name="y_codes%d" % h, align_bytes=64) for h in range(2)]
 
-        def weave(copy, i, first=0, last=None):
+        def weave(copy, i):
             h, a, b = pieces[i]
-            runs = slice(first, last)
-            copy(y_bf[i][:].rearrange("p (c i t) -> p c t i", i=4, t=PACK)[:, runs], y[h][:, :, a:b].rearrange("p t (c i) -> p c t i", i=4)[:, runs])
+            copy(y_bf[i][:].rearrange("p (c i t) -> p c t i", i=4, t=PACK), y[h][:, :, a:b].rearrange("p t (c i) -> p c t i", i=4))
 
         def quant_y(i):
             h, a, b = pieces[i]
@@ -173,10 +176,9 @@ def tile_picked_mingru8_none_po_kernel(tc, x_words, x_scales, w1, w2, st, offs, 
             nc.vector.tensor_tensor(y[1][:, 1:3, a:b], keep[1][:, 1:3, a:b], fresh[1][:, 1:3, a:b], ALU.subtract)
         nc.sync.dma_start(out_rows[:, 1:3, HALF:S], y[1][:, 1:3, :])
         weave(nc.scalar.copy, 1)
-        weave(nc.scalar.copy, 2, 0, SCALAR_RUNS)
         quant_y(0)
         nc.scalar.dma_start(out_words[:, 0:HALF], y_codes[0][:].bitcast(I32))
-        weave(nc.vector.tensor_copy, 2, SCALAR_RUNS)
+        weave(nc.vector.tensor_copy, 2)
         quant_y(1)
         quant_y(2)
         nc.scalar.dma_start(out_words[:, HALF:S], y_codes[1][:].bitcast(I32))

from contextlib import ExitStack

import concourse.mybir as mybir

K, T, S, N = 512, 2048, 512, 512
FLOPS = 2 * 2 * K * N * S

F32 = mybir.dt.float32
BF16 = mybir.dt.bfloat16
I32 = mybir.dt.int32
U32 = mybir.dt.uint32
U16 = mybir.dt.uint16
U8 = mybir.dt.uint8
FP8X4 = mybir.dt.float8_e4m3fn_x4
ALU = mybir.AluOpType
ACT = mybir.ActivationFunctionType

P = 128
PACK = 4
HALF = S // 2
QUARTER = S // 4
W2_FIRST = 320


def tile_picked_mingru8_none_po_kernel(tc, x_words, x_scales, w1, w2, st, offs, par, out_0, out_1, out_2):
    nc = tc.nc
    with ExitStack() as ctx:
        sb = ctx.enter_context(tc.tile_pool(name="sb", bufs=1))
        ps = ctx.enter_context(tc.psum_pool(name="ps", bufs=1))

        par_t = sb.tile([P, S // 16], U16, name="par_t")
        offs_t = sb.tile([P, S // 16], U16, name="offs_t")
        x_w = sb.tile([P, T], U32, name="x_w", align_bytes=64)
        x_s = sb.tile([P, T], U8, name="x_s", align_bytes=64)
        st_t = [sb.tile([P, S], F32, name="st%d" % t, tag="st%d" % t, align_bytes=64) for t in range(PACK)]
        w_pieces = [[(0, 2, 0, N), (2, PACK, 0, N)], [(0, PACK, 0, W2_FIRST), (0, PACK, W2_FIRST, N)]]
        raw = [[sb.tile([P, j1 - j0, b - a], F32, name="raw%d%d" % (w, h), align_bytes=64) for h, (j0, j1, a, b) in enumerate(pieces)] for w, pieces in enumerate(w_pieces)]
        st_rows = st.rearrange("(p t) j -> p t j", t=PACK)
        w_rows = [w.rearrange("(p j) m -> p j m", j=PACK) for w in (w1, w2)]

        def load_w(w, h):
            j0, j1, a, b = w_pieces[w][h]
            nc.sync.dma_start(raw[w][h][:], w_rows[w][:, j0:j1, a:b])

        nc.vector.memset(x_s[:].bitcast(I32), 0)

        load_w(0, 0)
        nc.sync.dma_start(offs_t[:], offs)
        for q in range(4):
            nc.sync.dma_start(x_s[32 * q : 32 * q + 4, :].bitcast(I32), x_scales[0, 4 * q : 4 * q + 4, :].bitcast(I32))
        load_w(0, 1)
        nc.sync.dma_start(x_w[:].bitcast(I32), x_words[0].rearrange("p n r -> p (n r)").bitcast(I32))
        for h in range(2):
            load_w(1, h)
        nc.sync.dma_start(par_t[:], par)
        for t in range(PACK):
            nc.sync.dma_start(st_t[t][:], st_rows[:, t, :])

        w_bf = [sb.tile([P, PACK * N], BF16, name="w_bf%d" % w, align_bytes=64) for w in range(2)]
        w_codes = [sb.tile([P, N], U32, name="w_codes%d" % w, align_bytes=64) for w in range(2)]
        w_scales = [sb.tile([P, N], U8, name="w_scales%d" % w, align_bytes=64) for w in range(2)]

        def deal(copy, w, h, t0=0, t1=PACK):
            j0, j1, a, b = w_pieces[w][h]
            dst = w_bf[w][:].rearrange("p (t m j) -> p m j t", t=PACK, j=PACK)[:, a // PACK : b // PACK, j0:j1, t0:t1]
            src = raw[w][h][:].rearrange("p j (m t) -> p m j t", t=PACK)[:, :, :, t0:t1]
            copy(dst, src)

        def quant_w(w, t0=0, t1=PACK):
            cols = slice(P * t0, P * t1)
            nc.vector.quantize_mx(out=w_codes[w][:, cols].bitcast(FP8X4), scales=w_scales[w][:, cols], in_=w_bf[w][:, PACK * P * t0 : PACK * P * t1])

        xg_w = [sb.tile([P, HALF], U32, name="xg_w%d" % h, align_bytes=64) for h in range(2)]
        token_cuts = [(0, 0, QUARTER), (0, QUARTER, HALF), (1, 0, HALF)]
        xg_s = sb.tile([P, S], U8, name="xg_s", align_bytes=64)

        def products(w, h, t0, t1, a=0, b=HALF):
            bank = ps.tile([P, t1 - t0, b - a], F32, name="bank%d%d%d%d" % (w, h, t0, a))
            for t in range(t0, t1):
                cols = slice(P * t, P * (t + 1))
                nc.tensor.matmul_mx(
                    out=bank[:, t - t0, :],
                    lhsT=w_codes[w][:, cols].bitcast(FP8X4),
                    lhsT_scale=w_scales[w][:, cols],
                    rhs=xg_w[h][:, a:b].bitcast(FP8X4),
                    rhs_scale=xg_s[:, HALF * h + a : HALF * h + b],
                    start=True,
                    stop=True,
                )
            return bank

        def listed(t, h):
            return st_t[t][:].indirect(par_t[:, 16 * h : 16 * (h + 1)])

        for h in range(2):
            deal(nc.scalar.copy, 0, h, 0, 2)
        deal(nc.vector.tensor_copy, 0, 0, 2, PACK)
        nc.vector.tensor_copy(xg_s[:], x_s[:].indirect(offs_t[:]))
        deal(nc.vector.tensor_copy, 0, 1, 2, PACK)
        for pair in range(2):
            quant_w(0, 2 * pair, 2 * pair + 2)
        for h, a, b in token_cuts:
            nc.vector.tensor_copy(xg_w[h][:, a:b], x_w[:].indirect(offs_t[:, (HALF * h + a) // 16 : (HALF * h + b) // 16]))

        units = [(h, pair) for h in range(2) for pair in range(2)]
        u_first = [products(0, 0, 0, PACK, a, b) for h, a, b in token_cuts[:2]]
        u_bank = [products(0, 1, 2 * pair, 2 * pair + 2) for pair in range(2)]
        gate = [sb.tile([P, PACK, HALF], F32, name="gate%d" % h, align_bytes=64) for h in range(2)]
        fresh = [sb.tile([P, PACK, HALF], F32, name="fresh%d" % h, align_bytes=64) for h in range(2)]
        keep = [sb.tile([P, PACK, HALF], F32, name="keep%d" % h, align_bytes=64) for h in range(2)]
        picked = sb.tile([P, PACK, HALF], F32, name="picked", align_bytes=64)

        def make_gate(dst, bank):
            nc.scalar.activation(dst, bank[:], ACT.Sigmoid, scale=-1.0)

        def make_fresh(h, pair):
            planes = slice(2 * pair, 2 * pair + 2)
            nc.vector.scalar_tensor_tensor(fresh[h][:, planes, :], gate[h][:, planes, :], 1.0, c_bank[(h, pair)][:], ALU.subtract, ALU.mult)

        def gather_state(dst, t, h):
            nc.scalar.activation(dst, listed(t, h), ACT.Copy)

        for bank, (h, a, b) in zip(u_first, token_cuts):
            make_gate(gate[0][:, :, a:b], bank)
        for pair in range(2):
            make_gate(gate[1][:, 2 * pair : 2 * pair + 2, :], u_bank[pair])
        for t in range(1, PACK):
            gather_state(picked[:, t - 1, :], t, 0)
        gather_state(picked[:, 3, :], 3, 1)
        y = [sb.tile([P, PACK, HALF], F32, name="y%d" % h, tag=tag, align_bytes=64)[:] for h, tag in enumerate(("st3", "y1"))]
        second = [picked[:, 1, :], gate[0][:, 2, :], picked[:, 2, :], picked[:, 3, :]]

        deal(nc.vector.tensor_copy, 1, 0)
        for pair in range(2):
            deal(nc.vector.tensor_copy, 1, 1, 2 * pair, 2 * pair + 2)
        for pair in range(2):
            quant_w(1, 2 * pair, 2 * pair + 2)
        c_bank = {(h, pair): products(1, h, 2 * pair, 2 * pair + 2) for h, pair in units}
        nc.vector.tensor_tensor(keep[0][:, 0, :], listed(0, 0), gate[0][:, 0, :], ALU.mult)
        for t in (1, 2):
            nc.gpsimd.tensor_tensor(keep[0][:, t, :], gate[0][:, t, :], picked[:, t - 1, :], ALU.mult)
        for u in units:
            make_fresh(*u)
        for t in range(2):
            gather_state(second[t], t, 1)

        y_scales = sb.tile([P, S], U8, name="y_scales", align_bytes=64)
        out_rows = out_0.rearrange("(p t) j -> p t j", t=PACK)
        out_words = out_1[0].rearrange("p n r -> p (n r)").bitcast(I32)
        pieces = [(0, 0, HALF), (1, 0, QUARTER), (1, QUARTER, HALF)]
        y_bf = [sb.tile([P, PACK * (b - a)], BF16, name="y_bf%d" % i, align_bytes=64) for i, (h, a, b) in enumerate(pieces)]
        y_codes = [sb.tile([P, HALF], U32, name="y_codes%d" % h, align_bytes=64) for h in range(2)]

        def weave(copy, i):
            h, a, b = pieces[i]
            copy(y_bf[i][:].rearrange("p (c i t) -> p c t i", i=4, t=PACK), y[h][:, :, a:b].rearrange("p t (c i) -> p c t i", i=4))

        def quant_y(i):
            h, a, b = pieces[i]
            nc.vector.quantize_mx(out=y_codes[h][:, a:b].bitcast(FP8X4), scales=y_scales[:, HALF * h + a : HALF * h + b], in_=y_bf[i][:])

        nc.vector.tensor_tensor(keep[0][:, 3, :], gate[0][:, 3, :], picked[:, 2, :], ALU.mult)
        gather_state(picked[:, 2, :], 2, 1)
        for planes in (slice(0, 1), slice(1, PACK)):
            nc.vector.tensor_tensor(y[0][:, planes, :], keep[0][:, planes, :], fresh[0][:, planes, :], ALU.subtract)
        nc.sync.dma_start(out_rows[:, :, 0:HALF], y[0])
        weave(nc.scalar.copy, 0)
        outer = slice(0, PACK, PACK - 1)
        nc.vector.tensor_tensor(keep[1][:, outer, :], gate[1][:, outer, :], picked[:, 1:PACK:2, :], ALU.mult)
        nc.vector.tensor_tensor(keep[1][:, 1, :], gate[1][:, 1, :], second[1], ALU.mult)
        nc.vector.tensor_tensor(y[1][:, 3, :], keep[1][:, 3, :], fresh[1][:, 3, :], ALU.subtract)
        nc.vector.tensor_tensor(keep[1][:, 2, :], gate[1][:, 2, :], second[2], ALU.mult)
        nc.vector.tensor_tensor(y[1][:, 0, :], keep[1][:, 0, :], fresh[1][:, 0, :], ALU.subtract)
        nc.sync.dma_start(out_rows[:, outer, HALF:S], y[1][:, outer, :])
        for h, a, b in pieces[1:]:
            nc.vector.tensor_tensor(y[1][:, 1:3, a:b], keep[1][:, 1:3, a:b], fresh[1][:, 1:3, a:b], ALU.subtract)
        nc.sync.dma_start(out_rows[:, 1:3, HALF:S], y[1][:, 1:3, :])
        weave(nc.scalar.copy, 1)
        quant_y(0)
        nc.scalar.dma_start(out_words[:, 0:HALF], y_codes[0][:].bitcast(I32))
        weave(nc.vector.tensor_copy, 2)
        quant_y(1)
        quant_y(2)
        nc.scalar.dma_start(out_words[:, HALF:S], y_codes[1][:].bitcast(I32))
        for q in range(4):
            queue = nc.scalar if q == 0 else nc.sync
            queue.dma_start(out_2[0, 4 * q : 4 * q + 4, :].bitcast(I32), y_scales[32 * q : 32 * q + 4, :].bitcast(I32))
